import numpy as np
import ml_dtypes


def mxq(x, axis, fmt="e4m3"):
    dtype, down = {"e4m3": (ml_dtypes.float8_e4m3fn, 7), "e5m2": (ml_dtypes.float8_e5m2, 14)}[fmt]
    v = np.moveaxis(np.asarray(x, np.float32).astype(ml_dtypes.bfloat16).astype(np.float64), axis, -1)
    blocks = v.reshape(v.shape[:-1] + (-1, 32))
    amax = np.abs(blocks).max(-1, keepdims=True)
    byte = np.maximum(np.where(amax > 0, np.frexp(amax)[1] - 1 + 127, 0) - down, 1)
    scale = np.exp2(byte - 127.0)
    codes = (blocks / scale).astype(np.float32).astype(dtype).astype(np.float64)
    return np.moveaxis((codes * scale).reshape(v.shape), -1, axis)


WIDE = False


def mx_kscale(k):
    if not WIDE:
        return np.ones(k)
    levels = np.array([10, -10, 5, -5, 0])
    if k % 512:
        return np.exp2(np.random.permutation(np.resize(levels, k // 32))).repeat(32)
    a = np.empty((k // 512, 16))
    for p in range(k // 512):
        a[p, :8] = np.random.permutation(np.resize(levels, 8))
        for g in range(8):
            far = levels[np.abs(levels - a[p, g]) >= 10]
            a[p, g + 8] = far[np.random.randint(len(far))]
    return np.exp2(a.ravel()).repeat(32)


def f64(x):
    return np.asarray(x).astype(np.float64)


def striped(idx):
    return np.tile(np.asarray(idx).reshape(-1, 16).T, (8, 1)).astype(np.uint16)


def unstriped(offs):
    return offs[:16].T.reshape(-1).astype(np.int64)


E2M1 = np.array([0.0, 0.5, 1.0, 1.5, 2.0, 3.0, 4.0, 6.0, -0.0, -0.5, -1.0, -1.5, -2.0, -3.0, -4.0, -6.0])


def pack_weight(w, fmt):
    k, n = w.shape
    w = f64(np.asarray(w, np.float32).astype(ml_dtypes.bfloat16)).reshape(k // 32, 32, n)
    amax = np.abs(w).max(1)
    if fmt == "e4m3":
        byte = np.frexp(amax)[1] - 1 + 127 - 7
    else:
        mant, ex = np.frexp(amax / 6.0)
        byte = np.where(mant > 0.5, ex, ex - 1) + 127
    byte = np.clip(np.where(amax > 0, byte, 1), 1, 254)
    scaled = (w * np.exp2(127.0 - byte)[:, None, :]).reshape(k, n).astype(np.float32)
    by_word = np.ascontiguousarray(scaled.reshape(k // 512, 128, 4, n).transpose(0, 1, 3, 2))
    if fmt == "e4m3":
        words = by_word.astype(ml_dtypes.float8_e4m3fn).view(np.uint8)
    else:
        c = by_word.astype(ml_dtypes.float4_e2m1fn).view(np.uint8) & 0xF
        words = (c[..., 0::2] | (c[..., 1::2] << 4)).reshape(k // 512, 128, 2 * n)
    return np.ascontiguousarray(words), np.ascontiguousarray(byte.astype(np.uint8).reshape(k // 512, 16, n))


def unpack_weight(words, scales, fmt):
    g, _, n = scales.shape
    words = np.ascontiguousarray(words).reshape(g, 128, n, -1)
    if fmt == "e4m3":
        vals = words.view(ml_dtypes.float8_e4m3fn).astype(np.float64)
    else:
        nib = np.empty((g, 128, n, 4), np.uint8)
        nib[..., 0::2] = words & 0xF
        nib[..., 1::2] = words >> 4
        vals = E2M1[nib]
    vals = vals * np.repeat(np.exp2(scales.astype(np.float64) - 127.0), 8, axis=1)[..., None]
    return vals.transpose(0, 1, 3, 2).reshape(g * 512, n)


D, T, I, Q, E = 512, 2048, 512, 128, 512


def setup_inputs():
    n = np.random.standard_normal
    idx = np.random.permutation(T)[:I]
    fd = mx_kscale(D)
    fi = mx_kscale(I)
    ti = np.ones(T)
    ti[idx] = fi
    keysp = pack_weight(n((D, T)) / fd[:, None], "e4m3")
    return {
        "query": (n((D, Q)) * 0.4 / np.sqrt(D) * fd[:, None]).astype(np.float32),
        "keys_words": keysp[0],
        "keys_scales": keysp[1],
        "c0": (np.random.uniform(0.5, 1.5, (Q, 1))).astype(np.float32),
        "c1": (np.random.uniform(-0.5, 0.7, (Q, 1))).astype(np.float32),
        "c2": (np.random.uniform(-0.5, 0.5, (Q, 1))).astype(np.float32),
        "size": (np.random.uniform(0.5, 2.0, (1, I)) * fi).astype(np.float32),
        "vals": (n((E, T)) / ti).astype(np.float32),
        "offs": striped(idx),
    }


def reference(query, keys_words, keys_scales, c0, c1, c2, size, vals, offs):
    idx = unstriped(offs)
    keysu = unpack_weight(keys_words, keys_scales, "e4m3")
    queryq = mxq(f64(query), 0, "e4m3")
    keysidxg = keysu[:, idx]
    a = queryq.T @ keysidxg
    a1 = np.pad(a, ((0, 0), (1, 0)))[:, :I]
    a2 = np.pad(a, ((0, 0), (2, 0)))[:, :I]
    s = f64(c0) * a + f64(c1) * a1 + f64(c2) * a2
    p = np.exp(s - np.max(s, axis=1, keepdims=True))
    w = p * f64(size) / np.sum(p, axis=1, keepdims=True)
    wt = w.T
    vt = f64(vals)[:, idx].T
    wtq = mxq(wt, 0, "e4m3")
    vtq = mxq(vt, 0, "e4m3")
    o = wtq.T @ vtq
    return o

@@ -1,0 +1,135 @@
+from contextlib import ExitStack
+
+import concourse.mybir as mybir
+from concourse.masks import make_identity
+
+D, T, I, Q, E = 512, 2048, 512, 128, 512
+FLOPS = 2 * D * Q * I + 2 * I * Q * E
+
+F32 = mybir.dt.float32
+BF16 = mybir.dt.bfloat16
+I32 = mybir.dt.int32
+U32 = mybir.dt.uint32
+U16 = mybir.dt.uint16
+U8 = mybir.dt.uint8
+FP8X4 = mybir.dt.float8_e4m3fn_x4
+ALU = mybir.AluOpType
+ACT = mybir.ActivationFunctionType
+P = 128
+PACK = 4
+
+
+def tile_attend_multitoken_kernel(tc, query, keys_words, keys_scales, c0, c1, c2, size, vals, offs, out):
+    nc = tc.nc
+    with ExitStack() as ctx:
+        sb = ctx.enter_context(tc.tile_pool(name="sb", bufs=1))
+        ps = ctx.enter_context(tc.psum_pool(name="ps", bufs=1))
+
+        key_words = sb.tile([P, T], U32, name="key_words")
+        key_scales = sb.tile([P, T], U8, name="key_scales")
+        offsets = sb.tile([P, I // 16], U16, name="offsets")
+        q_raw = sb.tile([P, PACK, Q], F32, name="q_raw")
+        mix = [sb.tile([P, 1], F32, name="mix%d" % k) for k in range(3)]
+        size_col = sb.tile([P, PACK], F32, name="size_col")
+        ident = sb.tile([P, P], F32, name="ident")
+        warm_in = sb.tile([P, 1], F32, name="warm_in")
+        warm_out = sb.tile([P, 1], F32, name="warm_out")
+
+        nc.vector.memset(key_scales[:].bitcast(I32), 0)
+        nc.vector.memset(warm_in[:], 0.0)
+        nc.scalar.activation(out=warm_out[:], in_=warm_in[:], func=ACT.Exp)
+
+        nc.sync.dma_start(out=q_raw[:], in_=query.rearrange("(p j) q -> p j q", j=PACK))
+        nc.sync.dma_start(offsets[:], offs)
+        nc.sync.dma_start(out=mix[0][:], in_=c0)
+        rows = keys_scales[0].rearrange("(g r) t -> r g t", r=4)
+        for r in range(4):
+            nc.sync.dma_start(out=key_scales[r:P:32, :].bitcast(I32), in_=rows[r].bitcast(I32))
+        nc.sync.dma_start(out=key_words[:].bitcast(I32), in_=keys_words[0].rearrange("p n t -> p (n t)").bitcast(I32))
+
+        def load_values(j):
+            pool = sb.tile([P, T], F32, name="vals%d" % j, tag="slot%d" % j, align_bytes=64)
+            nc.sync.dma_start(out=pool[:], in_=vals[j * P:(j + 1) * P, :])
+            return pool
+
+        nc.sync.dma_start(out=mix[1][:], in_=c1)
+        pools = [load_values(0)]
+        nc.sync.dma_start(out=mix[2][:], in_=c2)
+        nc.sync.dma_start(out=size_col[:], in_=size.rearrange("o (p t) -> (o p) t", t=PACK))
+        pools.extend(load_values(j) for j in range(1, E // P))
+        make_identity(nc, ident[:])
+
+        def quantize(grouped, name, tag):
+            width = grouped.shape[1]
+            codes = sb.tile([P, width], U32, name=name + "_codes", tag=tag, align_bytes=64)
+            scales = sb.tile([P, width], U8, name=name + "_scales", align_bytes=64)
+            nc.vector.quantize_mx(out=codes[:].bitcast(FP8X4), scales=scales[:], in_=grouped[:].rearrange("p w j -> p (w j)"))
+            return codes, scales
+
+        def turn(rows_bf16, name, bank):
+            words = rows_bf16[:].bitcast(F32)
+            turned = ps.tile([P, 2, P], F32, name=name + "_turned", tag=bank)
+            for u in range(2):
+                nc.tensor.transpose(turned[:, u, :], words[:, u:I // 2:2], ident[:])
+            grouped = sb.tile([P, P, PACK], BF16, name=name + "_grouped", tag=name + "_grouped", align_bytes=64)
+            nc.scalar.copy(out=grouped[:].bitcast(F32), in_=turned[:].rearrange("p u r -> p r u"))
+            return grouped
+
+        k_codes = sb.tile([P, I], U32, name="k_codes", align_bytes=64)
+        k_scales = sb.tile([P, I], U8, name="k_scales", align_bytes=64)
+        nc.vector.tensor_copy(k_scales[:], key_scales[:].indirect(offsets[:]))
+
+        q_grouped = sb.tile([P, Q, PACK], BF16, name="q_grouped", align_bytes=64)
+        nc.scalar.copy(out=q_grouped[:], in_=q_raw[:].rearrange("p j q -> p q j"))
+        q_codes, q_scales = quantize(q_grouped, "q", "q_codes")
+        nc.vector.tensor_copy(k_codes[:], key_words[:].indirect(offsets[:]))
+
+        def gather_and_turn(j, bank, tag):
+            picked = sb.tile([P, I], BF16, name="picked%d" % j, tag=tag, align_bytes=64)
+            nc.vector.tensor_copy(picked[:], pools[j][:].indirect(offsets[:]))
+            return turn(picked, "v%d" % j, bank)
+
+        scores = ps.tile([Q, I], F32, name="scores", tag="scores")
+        nc.tensor.matmul_mx(out=scores[:], lhsT=q_codes[:].bitcast(FP8X4), lhsT_scale=q_scales[:],
+                            rhs=k_codes[:].bitcast(FP8X4), rhs_scale=k_scales[:], start=True, stop=True)
+
+        size_rows = ps.tile([Q, PACK, P], F32, name="size_rows")
+        for t in range(PACK):
+            nc.tensor.transpose(size_rows[:, t, :], size_col[:, t:t + 1].to_broadcast([P, P]), ident[:])
+
+        v_grouped = [gather_and_turn(0, "turn0", "picked0")]
+        s = sb.tile([Q, I], F32, name="s", tag="s", align_bytes=64)
+        nc.scalar.activation(out=s[:], in_=scores[:], func=ACT.Copy, scale=mix[0][:])
+        for k in (2, 1):
+            nc.vector.scalar_tensor_tensor(out=s[:, k:], in0=scores[:, :I - k], scalar=mix[k][:], in1=s[:, k:],
+                                           op0=ALU.mult, op1=ALU.add)
+        neg_max = sb.tile([Q, 1], F32, name="neg_max")
+        neg_s = sb.tile([Q, I], F32, name="neg_s")
+        nc.vector.tensor_scalar(out=neg_s[:], in0=s[:], scalar1=-1.0, scalar2=None, op0=ALU.mult, op1=ALU.min, accum_out=neg_max[:])
+        p = sb.tile([Q, I], F32, name="p", tag="p", align_bytes=64)
+        row_sum = sb.tile([Q, 1], F32, name="row_sum")
+        nc.scalar.activation(out=p[:], in_=neg_s[:], func=ACT.Exp, scale=-1.0, bias=neg_max[:], accum_out=row_sum[:])
+        v_grouped.append(gather_and_turn(1, "turn1", "s"))
+        inv_sum = sb.tile([Q, 1], F32, name="inv_sum", tag="slot1", align_bytes=64)
+        nc.vector.reciprocal(out=inv_sum[:], in_=row_sum[:])
+        w = sb.tile([Q, I], BF16, name="w")
+        nc.vector.scalar_tensor_tensor(out=w[:].rearrange("q (p t) -> q p t", t=PACK), in0=p[:].rearrange("q (p t) -> q p t", t=PACK),
+                                       scalar=inv_sum[:], in1=size_rows[:].rearrange("q t p -> q p t"),
+                                       op0=ALU.mult, op1=ALU.mult)
+        w_grouped = turn(w, "w", "turn_w")
+        v_mx = [quantize(v_grouped[0], "v0", "p")]
+        v_grouped.append(gather_and_turn(2, "turn2", "v0_grouped"))
+        w_codes, w_scales = quantize(w_grouped, "w", "slot2")
+        v_mx.append(quantize(v_grouped[1], "v1", "w_grouped"))
+        v_grouped.append(gather_and_turn(3, "scores", "v1_grouped"))
+        v_mx.append(quantize(v_grouped[2], "v2", "slot3"))
+        v_mx.append(quantize(v_grouped[3], "v3", "v3_codes"))
+
+        for name, blocks in (("head", (0, 1)), ("tail", (2, 3))):
+            acc = ps.tile([Q, len(blocks), P], F32, name="acc_" + name)
+            for n, j in enumerate(blocks):
+                nc.tensor.matmul_mx(out=acc[:, n, :], lhsT=w_codes[:].bitcast(FP8X4), lhsT_scale=w_scales[:],
+                                    rhs=v_mx[j][0][:].bitcast(FP8X4), rhs_scale=v_mx[j][1][:], start=True, stop=True)
+            res = sb.tile([Q, len(blocks) * P], F32, name="res_" + name)
+            nc.scalar.copy(out=res[:], in_=acc[:].rearrange("q n e -> q (n e)"))
+            nc.sync.dma_start(out=out[:, blocks[0] * P:(blocks[-1] + 1) * P], in_=res[:])

@@ -17,119 +17,129 @@ ALU = mybir.AluOpType
 ACT = mybir.ActivationFunctionType
 P = 128
 PACK = 4
+POOL_BYTES = 4 * T
+SMALL = 32
+AT_V1 = 0
+AT_SMALL = POOL_BYTES
+AT_V0 = AT_SMALL + 4 * SMALL
+AT_V2 = AT_V0 + POOL_BYTES
+AT_V3 = AT_V2 + POOL_BYTES
+AT_VALS = (AT_V0, AT_V1, AT_V2, AT_V3)
 
 
 def tile_attend_multitoken_kernel(tc, query, keys_words, keys_scales, c0, c1, c2, size, vals, offs, out):
     nc = tc.nc
     with ExitStack() as ctx:
         sb = ctx.enter_context(tc.tile_pool(name="sb", bufs=1))
+        shared = ctx.enter_context(tc.tile_pool(name="shared", bufs=1))
         ps = ctx.enter_context(tc.psum_pool(name="ps", bufs=1))
 
-        key_words = sb.tile([P, T], U32, name="key_words")
+        key_words = shared.tile([P, T], U32, name="key_words", offset=AT_V3)
         key_scales = sb.tile([P, T], U8, name="key_scales")
         offsets = sb.tile([P, I // 16], U16, name="offsets")
-        q_raw = sb.tile([P, PACK, Q], F32, name="q_raw")
-        mix = [sb.tile([P, 1], F32, name="mix%d" % k) for k in range(3)]
-        size_col = sb.tile([P, PACK], F32, name="size_col")
+        q_raw = shared.tile([P, PACK, Q], F32, name="q_raw", offset=AT_V2)
+        warm = shared.tile([P, 6 * SMALL // 4], F32, name="warm", offset=AT_SMALL - SMALL)
         ident = sb.tile([P, P], F32, name="ident")
-        warm_in = sb.tile([P, 1], F32, name="warm_in")
-        warm_out = sb.tile([P, 1], F32, name="warm_out")
 
         nc.vector.memset(key_scales[:].bitcast(I32), 0)
-        nc.vector.memset(warm_in[:], 0.0)
-        nc.scalar.activation(out=warm_out[:], in_=warm_in[:], func=ACT.Exp)
+        nc.vector.memset(warm[:], 0.0)
+        nc.scalar.activation(out=warm[:], in_=warm[:], func=ACT.Exp)
+        make_identity(nc, ident[:])
 
-        nc.sync.dma_start(out=q_raw[:], in_=query.rearrange("(p j) q -> p j q", j=PACK))
+        def load_values(j):
+            pool = shared.tile([P, T], F32, name="vals%d" % j, offset=AT_VALS[j])
+            nc.sync.dma_start(out=pool[:], in_=vals[j * P:(j + 1) * P, :])
+            return pool
+
         nc.sync.dma_start(offsets[:], offs)
+        nc.sync.dma_start(out=key_words[:].bitcast(I32), in_=keys_words[0].rearrange("p n t -> p (n t)").bitcast(I32))
+        nc.sync.dma_start(out=q_raw[:], in_=query.rearrange("(p j) q -> p j q", j=PACK))
+        mix = [sb.tile([P, 1], F32, name="mix0")]
         nc.sync.dma_start(out=mix[0][:], in_=c0)
         rows = keys_scales[0].rearrange("(g r) t -> r g t", r=4)
         for r in range(4):
             nc.sync.dma_start(out=key_scales[r:P:32, :].bitcast(I32), in_=rows[r].bitcast(I32))
-        nc.sync.dma_start(out=key_words[:].bitcast(I32), in_=keys_words[0].rearrange("p n t -> p (n t)").bitcast(I32))
-
-        def load_values(j):
-            pool = sb.tile([P, T], F32, name="vals%d" % j, tag="slot%d" % j, align_bytes=64)
-            nc.sync.dma_start(out=pool[:], in_=vals[j * P:(j + 1) * P, :])
-            return pool
-
-        nc.sync.dma_start(out=mix[1][:], in_=c1)
+        mix.extend(shared.tile([P, 1], F32, name="mix%d" % k, offset=AT_SMALL + k * SMALL) for k in (1, 2))
+        size_col = shared.tile([P, PACK], F32, name="size_col", offset=AT_SMALL)
         pools = [load_values(0)]
         nc.sync.dma_start(out=mix[2][:], in_=c2)
+        nc.sync.dma_start(out=mix[1][:], in_=c1)
         nc.sync.dma_start(out=size_col[:], in_=size.rearrange("o (p t) -> (o p) t", t=PACK))
-        pools.extend(load_values(j) for j in range(1, E // P))
-        make_identity(nc, ident[:])
+        pools.append(load_values(1))
 
-        def quantize(grouped, name, tag):
-            width = grouped.shape[1]
-            codes = sb.tile([P, width], U32, name=name + "_codes", tag=tag, align_bytes=64)
-            scales = sb.tile([P, width], U8, name=name + "_scales", align_bytes=64)
-            nc.vector.quantize_mx(out=codes[:].bitcast(FP8X4), scales=scales[:], in_=grouped[:].rearrange("p w j -> p (w j)"))
-            return codes, scales
+        def quantize(grouped, codes, name):
+            scales = sb.tile([P, grouped.shape[1]], U8, name=name + "_scales", align_bytes=64)
+            nc.vector.quantize_mx(out=codes[:].bitcast(FP8X4), scales=scales[:], in_=grouped.rearrange("p w j -> p (w j)"))
+            return scales
 
-        def turn(rows_bf16, name, bank):
+        def turn(rows_bf16, grouped, name, bank):
             words = rows_bf16[:].bitcast(F32)
             turned = ps.tile([P, 2, P], F32, name=name + "_turned", tag=bank)
             for u in range(2):
                 nc.tensor.transpose(turned[:, u, :], words[:, u:I // 2:2], ident[:])
-            grouped = sb.tile([P, P, PACK], BF16, name=name + "_grouped", tag=name + "_grouped", align_bytes=64)
-            nc.scalar.copy(out=grouped[:].bitcast(F32), in_=turned[:].rearrange("p u r -> p r u"))
-            return grouped
+            nc.scalar.copy(out=grouped.bitcast(F32), in_=turned[:].rearrange("p u r -> p r u"))
 
         k_codes = sb.tile([P, I], U32, name="k_codes", align_bytes=64)
         k_scales = sb.tile([P, I], U8, name="k_scales", align_bytes=64)
+        nc.vector.tensor_copy(k_codes[:], key_words[:].indirect(offsets[:]))
         nc.vector.tensor_copy(k_scales[:], key_scales[:].indirect(offsets[:]))
-
         q_grouped = sb.tile([P, Q, PACK], BF16, name="q_grouped", align_bytes=64)
         nc.scalar.copy(out=q_grouped[:], in_=q_raw[:].rearrange("p j q -> p q j"))
-        q_codes, q_scales = quantize(q_grouped, "q", "q_codes")
-        nc.vector.tensor_copy(k_codes[:], key_words[:].indirect(offsets[:]))
-
-        def gather_and_turn(j, bank, tag):
-            picked = sb.tile([P, I], BF16, name="picked%d" % j, tag=tag, align_bytes=64)
-            nc.vector.tensor_copy(picked[:], pools[j][:].indirect(offsets[:]))
-            return turn(picked, "v%d" % j, bank)
+        q_codes = sb.tile([P, Q], U32, name="q_codes", align_bytes=64)
+        q_scales = quantize(q_grouped[:], q_codes, "q")
+        pools.extend([load_values(2), load_values(3)])
 
         scores = ps.tile([Q, I], F32, name="scores", tag="scores")
         nc.tensor.matmul_mx(out=scores[:], lhsT=q_codes[:].bitcast(FP8X4), lhsT_scale=q_scales[:],
                             rhs=k_codes[:].bitcast(FP8X4), rhs_scale=k_scales[:], start=True, stop=True)
-
-        size_rows = ps.tile([Q, PACK, P], F32, name="size_rows")
-        for t in range(PACK):
-            nc.tensor.transpose(size_rows[:, t, :], size_col[:, t:t + 1].to_broadcast([P, P]), ident[:])
-
-        v_grouped = [gather_and_turn(0, "turn0", "picked0")]
-        s = sb.tile([Q, I], F32, name="s", tag="s", align_bytes=64)
+        s = sb.tile([Q, I], F32, name="s")
         nc.scalar.activation(out=s[:], in_=scores[:], func=ACT.Copy, scale=mix[0][:])
+
+        def gather_values(j):
+            picked = sb.tile([P, I], BF16, name="picked%d" % j)
+            nc.vector.tensor_copy(picked[:], pools[j][:].indirect(offsets[:]))
+            return picked
+
+        early = sb.tile([P, 4 * P, PACK], BF16, name="early", align_bytes=64)
+        turn(gather_values(0), early[:, P:2 * P, :], "v0", "turn0")
         for k in (2, 1):
             nc.vector.scalar_tensor_tensor(out=s[:, k:], in0=scores[:, :I - k], scalar=mix[k][:], in1=s[:, k:],
                                            op0=ALU.mult, op1=ALU.add)
         neg_max = sb.tile([Q, 1], F32, name="neg_max")
-        neg_s = sb.tile([Q, I], F32, name="neg_s")
-        nc.vector.tensor_scalar(out=neg_s[:], in0=s[:], scalar1=-1.0, scalar2=None, op0=ALU.mult, op1=ALU.min, accum_out=neg_max[:])
-        p = sb.tile([Q, I], F32, name="p", tag="p", align_bytes=64)
+        nc.vector.tensor_reduce(out=neg_max[:], in_=s[:], axis=mybir.AxisListType.X, op=ALU.max, negate=True)
+        p = sb.tile([Q, I], F32, name="p")
         row_sum = sb.tile([Q, 1], F32, name="row_sum")
-        nc.scalar.activation(out=p[:], in_=neg_s[:], func=ACT.Exp, scale=-1.0, bias=neg_max[:], accum_out=row_sum[:])
-        v_grouped.append(gather_and_turn(1, "turn1", "s"))
-        inv_sum = sb.tile([Q, 1], F32, name="inv_sum", tag="slot1", align_bytes=64)
+        nc.scalar.activation(out=p[:], in_=s[:], func=ACT.Exp, bias=neg_max[:], accum_out=row_sum[:])
+
+        size_rows = ps.tile([Q, PACK, P], F32, name="size_rows", tag="scores")
+        for t in range(PACK):
+            nc.tensor.transpose(size_rows[:, t, :], size_col[:, t:t + 1].to_broadcast([P, P]), ident[:])
+        turn(gather_values(1), early[:, 2 * P:3 * P, :], "v1", "turn1")
+
+        inv_sum = sb.tile([Q, 1], F32, name="inv_sum")
         nc.vector.reciprocal(out=inv_sum[:], in_=row_sum[:])
         w = sb.tile([Q, I], BF16, name="w")
         nc.vector.scalar_tensor_tensor(out=w[:].rearrange("q (p t) -> q p t", t=PACK), in0=p[:].rearrange("q (p t) -> q p t", t=PACK),
                                        scalar=inv_sum[:], in1=size_rows[:].rearrange("q t p -> q p t"),
                                        op0=ALU.mult, op1=ALU.mult)
-        w_grouped = turn(w, "w", "turn_w")
-        v_mx = [quantize(v_grouped[0], "v0", "p")]
-        v_grouped.append(gather_and_turn(2, "turn2", "v0_grouped"))
-        w_codes, w_scales = quantize(w_grouped, "w", "slot2")
-        v_mx.append(quantize(v_grouped[1], "v1", "w_grouped"))
-        v_grouped.append(gather_and_turn(3, "scores", "v1_grouped"))
-        v_mx.append(quantize(v_grouped[2], "v2", "slot3"))
-        v_mx.append(quantize(v_grouped[3], "v3", "v3_codes"))
+        turn(w, early[:, 0:P, :], "w", "turn_w")
+        turn(gather_values(2), early[:, 3 * P:4 * P, :], "v2", "turn2")
+        v3_grouped = sb.tile([P, P, PACK], BF16, name="v3_grouped", align_bytes=64)
+        turn(gather_values(3), v3_grouped[:], "v3", "scores")
+        early_codes = shared.tile([P, 4 * P], U32, name="early_codes", offset=AT_V3, align_bytes=64)
+        early_scales = quantize(early[:], early_codes, "early")
+        v3_codes = sb.tile([P, P], U32, name="v3_codes", align_bytes=64)
+        v3_scales = quantize(v3_grouped[:], v3_codes, "v3")
 
-        for name, blocks in (("head", (0, 1)), ("tail", (2, 3))):
-            acc = ps.tile([Q, len(blocks), P], F32, name="acc_" + name)
-            for n, j in enumerate(blocks):
-                nc.tensor.matmul_mx(out=acc[:, n, :], lhsT=w_codes[:].bitcast(FP8X4), lhsT_scale=w_scales[:],
-                                    rhs=v_mx[j][0][:].bitcast(FP8X4), rhs_scale=v_mx[j][1][:], start=True, stop=True)
-            res = sb.tile([Q, len(blocks) * P], F32, name="res_" + name)
-            nc.scalar.copy(out=res[:], in_=acc[:].rearrange("q n e -> q (n e)"))
-            nc.sync.dma_start(out=out[:, blocks[0] * P:(blocks[-1] + 1) * P], in_=res[:])
+        head = ((early_codes[:, P:3 * P], early_scales[:, P:3 * P]), (early_codes[:, 3 * P:], early_scales[:, 3 * P:]))
+        for name, first, parts in (("head", 0, head), ("tail", 3 * P, ((v3_codes[:], v3_scales[:]),))):
+            width = sum(codes.shape[1] for codes, scales in parts)
+            acc = ps.tile([Q, width], F32, name="acc_" + name)
+            col = 0
+            for codes, scales in parts:
+                nc.tensor.matmul_mx(out=acc[:, col:col + codes.shape[1]], lhsT=early_codes[:, :P].bitcast(FP8X4), lhsT_scale=early_scales[:, :P],
+                                    rhs=codes.bitcast(FP8X4), rhs_scale=scales, start=True, stop=True)
+                col = col + codes.shape[1]
+            res = sb.tile([Q, width], F32, name="res_" + name)
+            nc.scalar.copy(out=res[:], in_=acc[:])
+            nc.sync.dma_start(out=out[:, first:first + width], in_=res[:])

@@ -19,10 +19,10 @@ P = 128
 PACK = 4
 POOL_BYTES = 4 * T
 SMALL = 32
-AT_V1 = 0
-AT_SMALL = POOL_BYTES
-AT_V0 = AT_SMALL + 4 * SMALL
-AT_V2 = AT_V0 + POOL_BYTES
+AT_SMALL = 0
+AT_V0 = 4 * SMALL
+AT_V1 = AT_V0 + POOL_BYTES
+AT_V2 = AT_V1 + POOL_BYTES
 AT_V3 = AT_V2 + POOL_BYTES
 AT_VALS = (AT_V0, AT_V1, AT_V2, AT_V3)
 
@@ -34,17 +34,20 @@ def tile_attend_multitoken_kernel(tc, query, keys_words, keys_scales, c0, c1, c2
         shared = ctx.enter_context(tc.tile_pool(name="shared", bufs=1))
         ps = ctx.enter_context(tc.psum_pool(name="ps", bufs=1))
 
-        key_words = shared.tile([P, T], U32, name="key_words", offset=AT_V3)
         key_scales = sb.tile([P, T], U8, name="key_scales")
         offsets = sb.tile([P, I // 16], U16, name="offsets")
-        q_raw = shared.tile([P, PACK, Q], F32, name="q_raw", offset=AT_V2)
-        warm = shared.tile([P, 6 * SMALL // 4], F32, name="warm", offset=AT_SMALL - SMALL)
+        q_raw = shared.tile([P, PACK, Q], F32, name="q_raw", offset=AT_SMALL)
+        zeros = shared.tile([P, P], F32, name="zeros", offset=AT_V3)
+        warm = sb.tile([P, 1], F32, name="warm")
         ident = sb.tile([P, P], F32, name="ident")
+        c0_col = sb.tile([P, 1], F32, name="c0_col")
 
+        nc.vector.memset(zeros[:], 0.0)
         nc.vector.memset(key_scales[:].bitcast(I32), 0)
+        nc.vector.tensor_copy(out=ident[:], in_=zeros[:])
         nc.vector.memset(warm[:], 0.0)
+        make_identity(nc, ident[:], nomemset=True)
         nc.scalar.activation(out=warm[:], in_=warm[:], func=ACT.Exp)
-        make_identity(nc, ident[:])
 
         def load_values(j):
             pool = shared.tile([P, T], F32, name="vals%d" % j, offset=AT_VALS[j])
@@ -52,20 +55,13 @@ def tile_attend_multitoken_kernel(tc, query, keys_words, keys_scales, c0, c1, c2
             return pool
 
         nc.sync.dma_start(offsets[:], offs)
-        nc.sync.dma_start(out=key_words[:].bitcast(I32), in_=keys_words[0].rearrange("p n t -> p (n t)").bitcast(I32))
         nc.sync.dma_start(out=q_raw[:], in_=query.rearrange("(p j) q -> p j q", j=PACK))
-        mix = [sb.tile([P, 1], F32, name="mix0")]
-        nc.sync.dma_start(out=mix[0][:], in_=c0)
+        nc.sync.dma_start(out=c0_col[:], in_=c0)
         rows = keys_scales[0].rearrange("(g r) t -> r g t", r=4)
         for r in range(4):
             nc.sync.dma_start(out=key_scales[r:P:32, :].bitcast(I32), in_=rows[r].bitcast(I32))
-        mix.extend(shared.tile([P, 1], F32, name="mix%d" % k, offset=AT_SMALL + k * SMALL) for k in (1, 2))
-        size_col = shared.tile([P, PACK], F32, name="size_col", offset=AT_SMALL)
-        pools = [load_values(0)]
-        nc.sync.dma_start(out=mix[2][:], in_=c2)
-        nc.sync.dma_start(out=mix[1][:], in_=c1)
-        nc.sync.dma_start(out=size_col[:], in_=size.rearrange("o (p t) -> (o p) t", t=PACK))
-        pools.append(load_values(1))
+        key_words = shared.tile([P, T], U32, name="key_words", offset=AT_V3)
+        nc.sync.dma_start(out=key_words[:].bitcast(I32), in_=keys_words[0].rearrange("p n t -> p (n t)").bitcast(I32))
 
         def quantize(grouped, codes, name):
             scales = sb.tile([P, grouped.shape[1]], U8, name=name + "_scales", align_bytes=64)
@@ -81,19 +77,26 @@ def tile_attend_multitoken_kernel(tc, query, keys_words, keys_scales, c0, c1, c2
 
         k_codes = sb.tile([P, I], U32, name="k_codes", align_bytes=64)
         k_scales = sb.tile([P, I], U8, name="k_scales", align_bytes=64)
-        nc.vector.tensor_copy(k_codes[:], key_words[:].indirect(offsets[:]))
         nc.vector.tensor_copy(k_scales[:], key_scales[:].indirect(offsets[:]))
-        q_grouped = sb.tile([P, Q, PACK], BF16, name="q_grouped", align_bytes=64)
+        q_grouped = shared.tile([P, Q, PACK], BF16, name="q_grouped", offset=AT_V2 - 64, align_bytes=64)
         nc.scalar.copy(out=q_grouped[:], in_=q_raw[:].rearrange("p j q -> p q j"))
+        pools = [load_values(0)]
+        mix = {}
+        for k, src in ((2, c2), (1, c1)):
+            mix[k] = shared.tile([P, 1], F32, name="mix%d" % k, offset=AT_SMALL + k * SMALL)
+            nc.sync.dma_start(out=mix[k][:], in_=src)
+        size_col = shared.tile([P, PACK], F32, name="size_col", offset=AT_SMALL)
+        nc.sync.dma_start(out=size_col[:], in_=size.rearrange("o (p t) -> (o p) t", t=PACK))
         q_codes = sb.tile([P, Q], U32, name="q_codes", align_bytes=64)
         q_scales = quantize(q_grouped[:], q_codes, "q")
-        pools.extend([load_values(2), load_values(3)])
+        nc.vector.tensor_copy(k_codes[:], key_words[:].indirect(offsets[:]))
+        pools.extend(load_values(j) for j in (1, 2, 3))
 
         scores = ps.tile([Q, I], F32, name="scores", tag="scores")
         nc.tensor.matmul_mx(out=scores[:], lhsT=q_codes[:].bitcast(FP8X4), lhsT_scale=q_scales[:],
                             rhs=k_codes[:].bitcast(FP8X4), rhs_scale=k_scales[:], start=True, stop=True)
         s = sb.tile([Q, I], F32, name="s")
-        nc.scalar.activation(out=s[:], in_=scores[:], func=ACT.Copy, scale=mix[0][:])
+        nc.scalar.activation(out=s[:], in_=scores[:], func=ACT.Copy, scale=c0_col[:])
 
         def gather_values(j):
             picked = sb.tile([P, I], BF16, name="picked%d" % j)
@@ -116,12 +119,13 @@ def tile_attend_multitoken_kernel(tc, query, keys_words, keys_scales, c0, c1, c2
             nc.tensor.transpose(size_rows[:, t, :], size_col[:, t:t + 1].to_broadcast([P, P]), ident[:])
         turn(gather_values(1), early[:, 2 * P:3 * P, :], "v1", "turn1")
 
-        inv_sum = sb.tile([Q, 1], F32, name="inv_sum")
+        sized = shared.tile([Q, I], F32, name="sized", offset=AT_V1)
+        nc.vector.tensor_tensor(out=sized[:].rearrange("q (p t) -> q p t", t=PACK), in0=size_rows[:].rearrange("q t p -> q p t"),
+                                in1=p[:].rearrange("q (p t) -> q p t", t=PACK), op=ALU.mult)
+        inv_sum = shared.tile([Q, 1], F32, name="inv_sum", offset=AT_V1 + 4 * I)
         nc.vector.reciprocal(out=inv_sum[:], in_=row_sum[:])
         w = sb.tile([Q, I], BF16, name="w")
-        nc.vector.scalar_tensor_tensor(out=w[:].rearrange("q (p t) -> q p t", t=PACK), in0=p[:].rearrange("q (p t) -> q p t", t=PACK),
-                                       scalar=inv_sum[:], in1=size_rows[:].rearrange("q t p -> q p t"),
-                                       op0=ALU.mult, op1=ALU.mult)
+        nc.scalar.activation(out=w[:], in_=sized[:], func=ACT.Copy, scale=inv_sum[:])
         turn(w, early[:, 0:P, :], "w", "turn_w")
         turn(gather_values(2), early[:, 3 * P:4 * P, :], "v2", "turn2")
         v3_grouped = sb.tile([P, P, PACK], BF16, name="v3_grouped", align_bytes=64)
@@ -131,15 +135,15 @@ def tile_attend_multitoken_kernel(tc, query, keys_words, keys_scales, c0, c1, c2
         v3_codes = sb.tile([P, P], U32, name="v3_codes", align_bytes=64)
         v3_scales = quantize(v3_grouped[:], v3_codes, "v3")
 
-        head = ((early_codes[:, P:3 * P], early_scales[:, P:3 * P]), (early_codes[:, 3 * P:], early_scales[:, 3 * P:]))
-        for name, first, parts in (("head", 0, head), ("tail", 3 * P, ((v3_codes[:], v3_scales[:]),))):
-            width = sum(codes.shape[1] for codes, scales in parts)
-            acc = ps.tile([Q, width], F32, name="acc_" + name)
-            col = 0
-            for codes, scales in parts:
-                nc.tensor.matmul_mx(out=acc[:, col:col + codes.shape[1]], lhsT=early_codes[:, :P].bitcast(FP8X4), lhsT_scale=early_scales[:, :P],
-                                    rhs=codes.bitcast(FP8X4), rhs_scale=scales, start=True, stop=True)
-                col = col + codes.shape[1]
-            res = sb.tile([Q, width], F32, name="res_" + name)
-            nc.scalar.copy(out=res[:], in_=acc[:])
-            nc.sync.dma_start(out=out[:, first:first + width], in_=res[:])
+        def product(first, codes, scales, copy, queue):
+            width = codes.shape[1]
+            acc = ps.tile([Q, width], F32, name="acc%d" % first)
+            nc.tensor.matmul_mx(out=acc[:], lhsT=early_codes[:, :P].bitcast(FP8X4), lhsT_scale=early_scales[:, :P],
+                                rhs=codes.bitcast(FP8X4), rhs_scale=scales, start=True, stop=True)
+            res = sb.tile([Q, width], F32, name="res%d" % first)
+            copy(out=res[:], in_=acc[:])
+            queue.dma_start(out=out[:, first:first + width], in_=res[:])
+
+        product(0, early_codes[:, P:3 * P], early_scales[:, P:3 * P], nc.scalar.copy, nc.sync)
+        product(2 * P, early_codes[:, 3 * P:], early_scales[:, 3 * P:], nc.vector.tensor_copy, nc.sync)
+        product(3 * P, v3_codes[:], v3_scales[:], nc.scalar.copy, nc.scalar)

@@ -18,13 +18,10 @@ ACT = mybir.ActivationFunctionType
 P = 128
 PACK = 4
 POOL_BYTES = 4 * T
-SMALL = 32
-AT_SMALL = 0
-AT_V0 = 4 * SMALL
-AT_V1 = AT_V0 + POOL_BYTES
-AT_V2 = AT_V1 + POOL_BYTES
-AT_V3 = AT_V2 + POOL_BYTES
-AT_VALS = (AT_V0, AT_V1, AT_V2, AT_V3)
+AT_VALS = tuple(j * POOL_BYTES for j in range(4))
+AT_PICKED0 = 4 * POOL_BYTES
+HALF = I // 2
+V3_ON_VECTOR = 288
 
 
 def tile_attend_multitoken_kernel(tc, query, keys_words, keys_scales, c0, c1, c2, size, vals, offs, out):
@@ -34,116 +31,125 @@ def tile_attend_multitoken_kernel(tc, query, keys_words, keys_scales, c0, c1, c2
         shared = ctx.enter_context(tc.tile_pool(name="shared", bufs=1))
         ps = ctx.enter_context(tc.psum_pool(name="ps", bufs=1))
 
-        key_scales = sb.tile([P, T], U8, name="key_scales")
+        q_raw = sb.tile([P, PACK, Q], F32, name="q_raw")
         offsets = sb.tile([P, I // 16], U16, name="offsets")
-        q_raw = shared.tile([P, PACK, Q], F32, name="q_raw", offset=AT_SMALL)
-        zeros = shared.tile([P, P], F32, name="zeros", offset=AT_V3)
-        warm = sb.tile([P, 1], F32, name="warm")
-        ident = sb.tile([P, P], F32, name="ident")
-        c0_col = sb.tile([P, 1], F32, name="c0_col")
-
-        nc.vector.memset(zeros[:], 0.0)
-        nc.vector.memset(key_scales[:].bitcast(I32), 0)
-        nc.vector.tensor_copy(out=ident[:], in_=zeros[:])
-        nc.vector.memset(warm[:], 0.0)
-        make_identity(nc, ident[:], nomemset=True)
-        nc.scalar.activation(out=warm[:], in_=warm[:], func=ACT.Exp)
-
-        def load_values(j):
-            pool = shared.tile([P, T], F32, name="vals%d" % j, offset=AT_VALS[j])
-            nc.sync.dma_start(out=pool[:], in_=vals[j * P:(j + 1) * P, :])
-            return pool
-
-        nc.sync.dma_start(offsets[:], offs)
         nc.sync.dma_start(out=q_raw[:], in_=query.rearrange("(p j) q -> p j q", j=PACK))
-        nc.sync.dma_start(out=c0_col[:], in_=c0)
+        nc.sync.dma_start(offsets[:], offs)
+
+        key_scales = sb.tile([P, T], U8, name="key_scales")
+        nc.vector.memset(key_scales[:].bitcast(I32), 0)
         rows = keys_scales[0].rearrange("(g r) t -> r g t", r=4)
         for r in range(4):
             nc.sync.dma_start(out=key_scales[r:P:32, :].bitcast(I32), in_=rows[r].bitcast(I32))
-        key_words = shared.tile([P, T], U32, name="key_words", offset=AT_V3)
+        key_words = sb.tile([P, T], U32, name="key_words")
         nc.sync.dma_start(out=key_words[:].bitcast(I32), in_=keys_words[0].rearrange("p n t -> p (n t)").bitcast(I32))
 
+        ident = sb.tile([P, P], F32, name="ident")
+        warm = sb.tile([P, 1], F32, name="warm")
+        nc.vector.memset(warm[:], 0.0)
+        nc.vector.memset(ident[:], 0.0)
+        make_identity(nc, ident[:], nomemset=True)
+        nc.scalar.activation(out=warm[:], in_=warm[:], func=ACT.Exp)
+
+        mix = []
+        for k, src in enumerate((c0, c1, c2)):
+            mix.append(sb.tile([P, 1], F32, name="mix%d" % k))
+            nc.sync.dma_start(out=mix[k][:], in_=src)
+        size_col = sb.tile([P, PACK], F32, name="size_col")
+        nc.sync.dma_start(out=size_col[:], in_=size.rearrange("o (p t) -> (o p) t", t=PACK))
+
+        pools = [shared.tile([P, T], F32, name="vals%d" % j, offset=at) for j, at in enumerate(AT_VALS)]
+        for j, pool in enumerate(pools):
+            nc.sync.dma_start(out=pool[:], in_=vals[j * P:(j + 1) * P, :])
+
         def quantize(grouped, codes, name):
-            scales = sb.tile([P, grouped.shape[1]], U8, name=name + "_scales", align_bytes=64)
+            scales = sb.tile([P, codes.shape[1]], U8, name=name + "_scales", align_bytes=64)
             nc.vector.quantize_mx(out=codes[:].bitcast(FP8X4), scales=scales[:], in_=grouped.rearrange("p w j -> p (w j)"))
             return scales
 
-        def turn(rows_bf16, grouped, name, bank):
-            words = rows_bf16[:].bitcast(F32)
+        def turn(words, grouped, name, bank, copy):
             turned = ps.tile([P, 2, P], F32, name=name + "_turned", tag=bank)
             for u in range(2):
                 nc.tensor.transpose(turned[:, u, :], words[:, u:I // 2:2], ident[:])
-            nc.scalar.copy(out=grouped.bitcast(F32), in_=turned[:].rearrange("p u r -> p r u"))
+            copy(out=grouped.bitcast(F32), in_=turned[:].rearrange("p u r -> p r u"))
 
+        def gather_values(j, picked, on_vector):
+            if on_vector > 0:
+                nc.vector.tensor_copy(picked[:, :on_vector], pools[j][:].indirect(offsets[:, :on_vector // 16]))
+            if on_vector < I:
+                nc.scalar.activation(out=picked[:, on_vector:], in_=pools[j][:].indirect(offsets[:, on_vector // 16:]), func=ACT.Copy)
+            return picked[:].bitcast(F32)
+
+        q_grouped = sb.tile([P, Q, PACK], BF16, name="q_grouped", align_bytes=64)
+        nc.scalar.copy(out=q_grouped[:], in_=q_raw[:].rearrange("p j q -> p q j"))
         k_codes = sb.tile([P, I], U32, name="k_codes", align_bytes=64)
         k_scales = sb.tile([P, I], U8, name="k_scales", align_bytes=64)
         nc.vector.tensor_copy(k_scales[:], key_scales[:].indirect(offsets[:]))
-        q_grouped = shared.tile([P, Q, PACK], BF16, name="q_grouped", offset=AT_V2 - 64, align_bytes=64)
-        nc.scalar.copy(out=q_grouped[:], in_=q_raw[:].rearrange("p j q -> p q j"))
-        pools = [load_values(0)]
-        mix = {}
-        for k, src in ((2, c2), (1, c1)):
-            mix[k] = shared.tile([P, 1], F32, name="mix%d" % k, offset=AT_SMALL + k * SMALL)
-            nc.sync.dma_start(out=mix[k][:], in_=src)
-        size_col = shared.tile([P, PACK], F32, name="size_col", offset=AT_SMALL)
-        nc.sync.dma_start(out=size_col[:], in_=size.rearrange("o (p t) -> (o p) t", t=PACK))
         q_codes = sb.tile([P, Q], U32, name="q_codes", align_bytes=64)
         q_scales = quantize(q_grouped[:], q_codes, "q")
-        nc.vector.tensor_copy(k_codes[:], key_words[:].indirect(offsets[:]))
-        pools.extend(load_values(j) for j in (1, 2, 3))
-
-        scores = ps.tile([Q, I], F32, name="scores", tag="scores")
-        nc.tensor.matmul_mx(out=scores[:], lhsT=q_codes[:].bitcast(FP8X4), lhsT_scale=q_scales[:],
-                            rhs=k_codes[:].bitcast(FP8X4), rhs_scale=k_scales[:], start=True, stop=True)
         s = sb.tile([Q, I], F32, name="s")
-        nc.scalar.activation(out=s[:], in_=scores[:], func=ACT.Copy, scale=c0_col[:])
-
-        def gather_values(j):
-            picked = sb.tile([P, I], BF16, name="picked%d" % j)
-            nc.vector.tensor_copy(picked[:], pools[j][:].indirect(offsets[:]))
-            return picked
-
-        early = sb.tile([P, 4 * P, PACK], BF16, name="early", align_bytes=64)
-        turn(gather_values(0), early[:, P:2 * P, :], "v0", "turn0")
-        for k in (2, 1):
-            nc.vector.scalar_tensor_tensor(out=s[:, k:], in0=scores[:, :I - k], scalar=mix[k][:], in1=s[:, k:],
-                                           op0=ALU.mult, op1=ALU.add)
-        neg_max = sb.tile([Q, 1], F32, name="neg_max")
-        nc.vector.tensor_reduce(out=neg_max[:], in_=s[:], axis=mybir.AxisListType.X, op=ALU.max, negate=True)
-        p = sb.tile([Q, I], F32, name="p")
-        row_sum = sb.tile([Q, 1], F32, name="row_sum")
-        nc.scalar.activation(out=p[:], in_=s[:], func=ACT.Exp, bias=neg_max[:], accum_out=row_sum[:])
-
-        size_rows = ps.tile([Q, PACK, P], F32, name="size_rows", tag="scores")
+        scores = {}
+        for first in (HALF, 0):
+            nc.vector.tensor_copy(k_codes[:, first:first + HALF], key_words[:].indirect(offsets[:, first // 16:(first + HALF) // 16]))
+            scores[first] = ps.tile([Q, HALF], F32, name="scores%d" % first, tag="scores%d" % first)
+            nc.tensor.matmul_mx(out=scores[first][:], lhsT=q_codes[:].bitcast(FP8X4), lhsT_scale=q_scales[:],
+                                rhs=k_codes[:, first:first + HALF].bitcast(FP8X4), rhs_scale=k_scales[:, first:first + HALF],
+                                start=True, stop=True)
+            nc.scalar.activation(out=s[:, first:first + HALF], in_=scores[first][:], func=ACT.Copy, scale=mix[0][:])
+        size_rows = ps.tile([Q, PACK, P], F32, name="size_rows")
         for t in range(PACK):
             nc.tensor.transpose(size_rows[:, t, :], size_col[:, t:t + 1].to_broadcast([P, P]), ident[:])
-        turn(gather_values(1), early[:, 2 * P:3 * P, :], "v1", "turn1")
-
-        sized = shared.tile([Q, I], F32, name="sized", offset=AT_V1)
-        nc.vector.tensor_tensor(out=sized[:].rearrange("q (p t) -> q p t", t=PACK), in0=size_rows[:].rearrange("q t p -> q p t"),
-                                in1=p[:].rearrange("q (p t) -> q p t", t=PACK), op=ALU.mult)
-        inv_sum = shared.tile([Q, 1], F32, name="inv_sum", offset=AT_V1 + 4 * I)
+        for k in (1, 2):
+            for first in (HALF, 0):
+                n = min(HALF, I - first - k)
+                nc.vector.scalar_tensor_tensor(out=s[:, first + k:first + k + n], in0=scores[first][:, :n], scalar=mix[k][:],
+                                               in1=s[:, first + k:first + k + n], op0=ALU.mult, op1=ALU.add)
+        neg_max = sb.tile([Q, 1], F32, name="neg_max")
+        nc.vector.tensor_reduce(out=neg_max[:], in_=s[:], axis=mybir.AxisListType.X, op=ALU.max, negate=True)
+        picked0 = gather_values(0, shared.tile([P, I], BF16, name="picked0", offset=AT_PICKED0), 0)
+        v0_grouped = sb.tile([P, P, PACK], BF16, name="v0_grouped", align_bytes=64)
+        turn(picked0, v0_grouped[:], "v0", "bank_c", nc.vector.tensor_copy)
+        p = shared.tile([Q, I], F32, name="p", offset=AT_VALS[0])
+        row_sum = sb.tile([Q, 1], F32, name="row_sum")
+        nc.scalar.activation(out=p[:], in_=s[:], func=ACT.Exp, bias=neg_max[:], accum_out=row_sum[:])
+        inv_sum = shared.tile([Q, 1], F32, name="inv_sum", offset=AT_PICKED0 + 32)
         nc.vector.reciprocal(out=inv_sum[:], in_=row_sum[:])
         w = sb.tile([Q, I], BF16, name="w")
-        nc.scalar.activation(out=w[:], in_=sized[:], func=ACT.Copy, scale=inv_sum[:])
-        turn(w, early[:, 0:P, :], "w", "turn_w")
-        turn(gather_values(2), early[:, 3 * P:4 * P, :], "v2", "turn2")
-        v3_grouped = sb.tile([P, P, PACK], BF16, name="v3_grouped", align_bytes=64)
-        turn(gather_values(3), v3_grouped[:], "v3", "scores")
-        early_codes = shared.tile([P, 4 * P], U32, name="early_codes", offset=AT_V3, align_bytes=64)
-        early_scales = quantize(early[:], early_codes, "early")
-        v3_codes = sb.tile([P, P], U32, name="v3_codes", align_bytes=64)
-        v3_scales = quantize(v3_grouped[:], v3_codes, "v3")
+        nc.vector.scalar_tensor_tensor(out=w[:].rearrange("q (p t) -> q p t", t=PACK), in0=p[:].rearrange("q (p t) -> q p t", t=PACK),
+                                       scalar=inv_sum[:], in1=size_rows[:].rearrange("q t p -> q p t"),
+                                       op0=ALU.mult, op1=ALU.mult)
+        picked1 = gather_values(1, sb.tile([P, I], BF16, name="picked1"), 0)
+        wv1_grouped = shared.tile([P, 2 * P, PACK], BF16, name="wv1_grouped", offset=AT_VALS[1], align_bytes=64)
+        turn(w[:].bitcast(F32), wv1_grouped[:, :P, :], "w", "scores0", nc.scalar.copy)
+        turn(picked1, wv1_grouped[:, P:, :], "v1", "size_rows", nc.scalar.copy)
+        picked2 = gather_values(2, sb.tile([P, I], BF16, name="picked2"), I)
+        v0_codes = shared.tile([P, P], U32, name="v0_codes", offset=AT_VALS[2] + 4 * 2 * P, align_bytes=64)
+        v0_scales = quantize(v0_grouped[:], v0_codes, "v0")
+        wv1_codes = shared.tile([P, 2 * P], U32, name="wv1_codes", offset=AT_VALS[2], align_bytes=64)
+        wv1_scales = quantize(wv1_grouped[:], wv1_codes, "wv1")
 
-        def product(first, codes, scales, copy, queue):
-            width = codes.shape[1]
-            acc = ps.tile([Q, width], F32, name="acc%d" % first)
-            nc.tensor.matmul_mx(out=acc[:], lhsT=early_codes[:, :P].bitcast(FP8X4), lhsT_scale=early_scales[:, :P],
+        def product(acc, codes, scales):
+            nc.tensor.matmul_mx(out=acc, lhsT=wv1_codes[:, :P].bitcast(FP8X4), lhsT_scale=wv1_scales[:, :P],
                                 rhs=codes.bitcast(FP8X4), rhs_scale=scales, start=True, stop=True)
-            res = sb.tile([Q, width], F32, name="res%d" % first)
-            copy(out=res[:], in_=acc[:])
-            queue.dma_start(out=out[:, first:first + width], in_=res[:])
 
-        product(0, early_codes[:, P:3 * P], early_scales[:, P:3 * P], nc.scalar.copy, nc.sync)
-        product(2 * P, early_codes[:, 3 * P:], early_scales[:, 3 * P:], nc.vector.tensor_copy, nc.sync)
-        product(3 * P, v3_codes[:], v3_scales[:], nc.scalar.copy, nc.scalar)
+        def store(first, acc, res, copy):
+            copy(out=res[:], in_=acc[:])
+            nc.sync.dma_start(out=out[:, first:first + res.shape[1]], in_=res[:])
+
+        acc01 = ps.tile([Q, 2 * P], F32, name="acc01")
+        product(acc01[:, :P], v0_codes[:], v0_scales[:])
+        product(acc01[:, P:], wv1_codes[:, P:], wv1_scales[:, P:])
+        picked3 = gather_values(3, sb.tile([P, I], BF16, name="picked3"), V3_ON_VECTOR)
+        v2_grouped = shared.tile([P, P, PACK], BF16, name="v2_grouped", offset=AT_VALS[3] + 4 * 2 * P, align_bytes=64)
+        turn(picked2, v2_grouped[:], "v2", "scores%d" % HALF, nc.vector.tensor_copy)
+        res01 = shared.tile([Q, 2 * P], F32, name="res01", offset=AT_VALS[3])
+        store(0, acc01, res01, nc.scalar.copy)
+        v3_grouped = sb.tile([P, P, PACK], BF16, name="v3_grouped", align_bytes=64)
+        turn(picked3, v3_grouped[:], "v3", "bank_c", nc.scalar.copy)
+        for j, grouped in ((2, v2_grouped), (3, v3_grouped)):
+            codes = sb.tile([P, P], U32, name="v%d_codes" % j, align_bytes=64)
+            scales = quantize(grouped[:], codes, "v%d" % j)
+            acc = ps.tile([Q, P], F32, name="acc%d" % j)
+            product(acc[:], codes[:], scales[:])
+            res = sb.tile([Q, P], F32, name="res%d" % j)
+            store(j * P, acc, res, nc.scalar.copy)

@@ -20,6 +20,7 @@ PACK = 4
 POOL_BYTES = 4 * T
 AT_VALS = tuple(j * POOL_BYTES for j in range(4))
 AT_PICKED0 = 4 * POOL_BYTES
+C1_ROW, C2_ROW = 4, 5
 HALF = I // 2
 V3_ON_VECTOR = 288
 
@@ -35,6 +36,8 @@ def tile_attend_multitoken_kernel(tc, query, keys_words, keys_scales, c0, c1, c2
         offsets = sb.tile([P, I // 16], U16, name="offsets")
         nc.sync.dma_start(out=q_raw[:], in_=query.rearrange("(p j) q -> p j q", j=PACK))
         nc.sync.dma_start(offsets[:], offs)
+        c0_col = sb.tile([P, 1], F32, name="c0_col")
+        nc.sync.dma_start(out=c0_col[:], in_=c0)
 
         key_scales = sb.tile([P, T], U8, name="key_scales")
         nc.vector.memset(key_scales[:].bitcast(I32), 0)
@@ -45,27 +48,24 @@ def tile_attend_multitoken_kernel(tc, query, keys_words, keys_scales, c0, c1, c2
         nc.sync.dma_start(out=key_words[:].bitcast(I32), in_=keys_words[0].rearrange("p n t -> p (n t)").bitcast(I32))
 
         ident = sb.tile([P, P], F32, name="ident")
+        small_rows = sb.tile([P, P], F32, name="small_rows")
         warm = sb.tile([P, 1], F32, name="warm")
         nc.vector.memset(warm[:], 0.0)
+        nc.vector.memset(small_rows[:], 0.0)
         nc.vector.memset(ident[:], 0.0)
         make_identity(nc, ident[:], nomemset=True)
         nc.scalar.activation(out=warm[:], in_=warm[:], func=ACT.Exp)
 
-        mix = []
-        for k, src in enumerate((c0, c1, c2)):
-            mix.append(sb.tile([P, 1], F32, name="mix%d" % k))
-            nc.sync.dma_start(out=mix[k][:], in_=src)
-        size_col = sb.tile([P, PACK], F32, name="size_col")
-        nc.sync.dma_start(out=size_col[:], in_=size.rearrange("o (p t) -> (o p) t", t=PACK))
+        for row, src in ((C1_ROW, c1), (C2_ROW, c2)):
+            nc.sync.dma_start(out=small_rows[row:row + 1, :], in_=src.rearrange("q o -> o q"))
+        nc.sync.dma_start(out=small_rows[0:PACK, :], in_=size.rearrange("o (t j) -> (o t) j", t=PACK))
 
         pools = [shared.tile([P, T], F32, name="vals%d" % j, offset=at) for j, at in enumerate(AT_VALS)]
         for j, pool in enumerate(pools):
             nc.sync.dma_start(out=pool[:], in_=vals[j * P:(j + 1) * P, :])
 
-        def quantize(grouped, codes, name):
-            scales = sb.tile([P, codes.shape[1]], U8, name=name + "_scales", align_bytes=64)
-            nc.vector.quantize_mx(out=codes[:].bitcast(FP8X4), scales=scales[:], in_=grouped.rearrange("p w j -> p (w j)"))
-            return scales
+        def quantize(grouped, codes, scales):
+            nc.vector.quantize_mx(out=codes.bitcast(FP8X4), scales=scales, in_=grouped.rearrange("p w j -> p (w j)"))
 
         def turn(words, grouped, name, bank, copy):
             turned = ps.tile([P, 2, P], F32, name=name + "_turned", tag=bank)
@@ -86,23 +86,29 @@ def tile_attend_multitoken_kernel(tc, query, keys_words, keys_scales, c0, c1, c2
         k_scales = sb.tile([P, I], U8, name="k_scales", align_bytes=64)
         nc.vector.tensor_copy(k_scales[:], key_scales[:].indirect(offsets[:]))
         q_codes = sb.tile([P, Q], U32, name="q_codes", align_bytes=64)
-        q_scales = quantize(q_grouped[:], q_codes, "q")
+        q_scales = sb.tile([P, Q], U8, name="q_scales", align_bytes=64)
+        quantize(q_grouped[:], q_codes[:], q_scales[:])
         s = sb.tile([Q, I], F32, name="s")
-        scores = {}
+        scores, small_turned = {}, {}
+        for first, name in ((HALF, "upper_bank"), (0, "lower_bank")):
+            bank = ps.tile([Q, HALF + P], F32, name=name)
+            scores[first], small_turned[first] = bank[:, :HALF], bank[:, HALF:]
+            nc.tensor.transpose(small_turned[first], small_rows[:], ident[:])
         for first in (HALF, 0):
             nc.vector.tensor_copy(k_codes[:, first:first + HALF], key_words[:].indirect(offsets[:, first // 16:(first + HALF) // 16]))
-            scores[first] = ps.tile([Q, HALF], F32, name="scores%d" % first, tag="scores%d" % first)
-            nc.tensor.matmul_mx(out=scores[first][:], lhsT=q_codes[:].bitcast(FP8X4), lhsT_scale=q_scales[:],
+            nc.tensor.matmul_mx(out=scores[first], lhsT=q_codes[:].bitcast(FP8X4), lhsT_scale=q_scales[:],
                                 rhs=k_codes[:, first:first + HALF].bitcast(FP8X4), rhs_scale=k_scales[:, first:first + HALF],
                                 start=True, stop=True)
-            nc.scalar.activation(out=s[:, first:first + HALF], in_=scores[first][:], func=ACT.Copy, scale=mix[0][:])
+            nc.scalar.activation(out=s[:, first:first + HALF], in_=scores[first], func=ACT.Copy, scale=c0_col[:])
+        size_cols = sb.tile([P, PACK], F32, name="size_cols")
+        nc.scalar.copy(out=size_cols[:], in_=small_turned[0][:, :PACK])
         size_rows = ps.tile([Q, PACK, P], F32, name="size_rows")
         for t in range(PACK):
-            nc.tensor.transpose(size_rows[:, t, :], size_col[:, t:t + 1].to_broadcast([P, P]), ident[:])
-        for k in (1, 2):
+            nc.tensor.transpose(size_rows[:, t, :], size_cols[:, t:t + 1].to_broadcast([P, P]), ident[:])
+        for k, row in ((1, C1_ROW), (2, C2_ROW)):
             for first in (HALF, 0):
                 n = min(HALF, I - first - k)
-                nc.vector.scalar_tensor_tensor(out=s[:, first + k:first + k + n], in0=scores[first][:, :n], scalar=mix[k][:],
+                nc.vector.scalar_tensor_tensor(out=s[:, first + k:first + k + n], in0=scores[first][:, :n], scalar=small_turned[first][:, row:row + 1],
                                                in1=s[:, first + k:first + k + n], op0=ALU.mult, op1=ALU.add)
         neg_max = sb.tile([Q, 1], F32, name="neg_max")
         nc.vector.tensor_reduce(out=neg_max[:], in_=s[:], axis=mybir.AxisListType.X, op=ALU.max, negate=True)
@@ -115,21 +121,25 @@ def tile_attend_multitoken_kernel(tc, query, keys_words, keys_scales, c0, c1, c2
         inv_sum = shared.tile([Q, 1], F32, name="inv_sum", offset=AT_PICKED0 + 32)
         nc.vector.reciprocal(out=inv_sum[:], in_=row_sum[:])
         w = sb.tile([Q, I], BF16, name="w")
-        nc.vector.scalar_tensor_tensor(out=w[:].rearrange("q (p t) -> q p t", t=PACK), in0=p[:].rearrange("q (p t) -> q p t", t=PACK),
-                                       scalar=inv_sum[:], in1=size_rows[:].rearrange("q t p -> q p t"),
+        nc.vector.scalar_tensor_tensor(out=w[:], in0=p[:],
+                                       scalar=inv_sum[:], in1=size_rows[:].rearrange("q t j -> q (t j)"),
                                        op0=ALU.mult, op1=ALU.mult)
         picked1 = gather_values(1, sb.tile([P, I], BF16, name="picked1"), 0)
-        wv1_grouped = shared.tile([P, 2 * P, PACK], BF16, name="wv1_grouped", offset=AT_VALS[1], align_bytes=64)
-        turn(w[:].bitcast(F32), wv1_grouped[:, :P, :], "w", "scores0", nc.scalar.copy)
-        turn(picked1, wv1_grouped[:, P:, :], "v1", "size_rows", nc.scalar.copy)
+        w_grouped = shared.tile([P, Q, PACK], BF16, name="w_grouped", offset=AT_VALS[1], align_bytes=64)
+        turn(w[:].bitcast(F32), w_grouped[:], "w", "lower_bank", nc.scalar.copy)
+        v1_grouped = sb.tile([P, P, PACK], BF16, name="v1_grouped", align_bytes=64)
+        turn(picked1, v1_grouped[:], "v1", "size_rows", nc.scalar.copy)
         picked2 = gather_values(2, sb.tile([P, I], BF16, name="picked2"), I)
-        v0_codes = shared.tile([P, P], U32, name="v0_codes", offset=AT_VALS[2] + 4 * 2 * P, align_bytes=64)
-        v0_scales = quantize(v0_grouped[:], v0_codes, "v0")
-        wv1_codes = shared.tile([P, 2 * P], U32, name="wv1_codes", offset=AT_VALS[2], align_bytes=64)
-        wv1_scales = quantize(wv1_grouped[:], wv1_codes, "wv1")
+        v01_codes = shared.tile([P, 2 * P], U32, name="v01_codes", offset=AT_VALS[2], align_bytes=64)
+        v01_scales = sb.tile([P, 2 * P], U8, name="v01_scales", align_bytes=64)
+        w_codes = shared.tile([P, Q], U32, name="w_codes", offset=AT_VALS[2] + 4 * 2 * P, align_bytes=64)
+        w_scales = sb.tile([P, Q], U8, name="w_scales", align_bytes=64)
+        quantize(v0_grouped[:], v01_codes[:, :P], v01_scales[:, :P])
+        quantize(w_grouped[:], w_codes[:], w_scales[:])
+        quantize(v1_grouped[:], v01_codes[:, P:], v01_scales[:, P:])
 
         def product(acc, codes, scales):
-            nc.tensor.matmul_mx(out=acc, lhsT=wv1_codes[:, :P].bitcast(FP8X4), lhsT_scale=wv1_scales[:, :P],
+            nc.tensor.matmul_mx(out=acc, lhsT=w_codes[:].bitcast(FP8X4), lhsT_scale=w_scales[:],
                                 rhs=codes.bitcast(FP8X4), rhs_scale=scales, start=True, stop=True)
 
         def store(first, acc, res, copy):
@@ -137,19 +147,19 @@ def tile_attend_multitoken_kernel(tc, query, keys_words, keys_scales, c0, c1, c2
             nc.sync.dma_start(out=out[:, first:first + res.shape[1]], in_=res[:])
 
         acc01 = ps.tile([Q, 2 * P], F32, name="acc01")
-        product(acc01[:, :P], v0_codes[:], v0_scales[:])
-        product(acc01[:, P:], wv1_codes[:, P:], wv1_scales[:, P:])
+        product(acc01[:], v01_codes[:], v01_scales[:])
         picked3 = gather_values(3, sb.tile([P, I], BF16, name="picked3"), V3_ON_VECTOR)
         v2_grouped = shared.tile([P, P, PACK], BF16, name="v2_grouped", offset=AT_VALS[3] + 4 * 2 * P, align_bytes=64)
-        turn(picked2, v2_grouped[:], "v2", "scores%d" % HALF, nc.vector.tensor_copy)
+        turn(picked2, v2_grouped[:], "v2", "upper_bank", nc.vector.tensor_copy)
         res01 = shared.tile([Q, 2 * P], F32, name="res01", offset=AT_VALS[3])
         store(0, acc01, res01, nc.scalar.copy)
         v3_grouped = sb.tile([P, P, PACK], BF16, name="v3_grouped", align_bytes=64)
         turn(picked3, v3_grouped[:], "v3", "bank_c", nc.scalar.copy)
-        for j, grouped in ((2, v2_grouped), (3, v3_grouped)):
+        for j, grouped, copy in ((2, v2_grouped, nc.scalar.copy), (3, v3_grouped, nc.vector.tensor_copy)):
             codes = sb.tile([P, P], U32, name="v%d_codes" % j, align_bytes=64)
-            scales = quantize(grouped[:], codes, "v%d" % j)
+            scales = sb.tile([P, P], U8, name="v%d_scales" % j, align_bytes=64)
+            quantize(grouped[:], codes[:], scales[:])
             acc = ps.tile([Q, P], F32, name="acc%d" % j)
             product(acc[:], codes[:], scales[:])
             res = sb.tile([Q, P], F32, name="res%d" % j)
-            store(j * P, acc, res, nc.scalar.copy)
+            store(j * P, acc, res, copy)

@@ -22,7 +22,8 @@ AT_VALS = tuple(j * POOL_BYTES for j in range(4))
 AT_PICKED0 = 4 * POOL_BYTES
 C1_ROW, C2_ROW = 4, 5
 HALF = I // 2
-V3_ON_VECTOR = 288
+LAST = P // 2
+V3_ON_VECTOR = 256
 
 
 def tile_attend_multitoken_kernel(tc, query, keys_words, keys_scales, c0, c1, c2, size, vals, offs, out):
@@ -49,12 +50,9 @@ def tile_attend_multitoken_kernel(tc, query, keys_words, keys_scales, c0, c1, c2
 
         ident = sb.tile([P, P], F32, name="ident")
         small_rows = sb.tile([P, P], F32, name="small_rows")
-        warm = sb.tile([P, 1], F32, name="warm")
-        nc.vector.memset(warm[:], 0.0)
         nc.vector.memset(small_rows[:], 0.0)
         nc.vector.memset(ident[:], 0.0)
         make_identity(nc, ident[:], nomemset=True)
-        nc.scalar.activation(out=warm[:], in_=warm[:], func=ACT.Exp)
 
         for row, src in ((C1_ROW, c1), (C2_ROW, c2)):
             nc.sync.dma_start(out=small_rows[row:row + 1, :], in_=src.rearrange("q o -> o q"))
@@ -153,13 +151,19 @@ def tile_attend_multitoken_kernel(tc, query, keys_words, keys_scales, c0, c1, c2
         turn(picked2, v2_grouped[:], "v2", "upper_bank", nc.vector.tensor_copy)
         res01 = shared.tile([Q, 2 * P], F32, name="res01", offset=AT_VALS[3])
         store(0, acc01, res01, nc.scalar.copy)
-        v3_grouped = sb.tile([P, P, PACK], BF16, name="v3_grouped", align_bytes=64)
-        turn(picked3, v3_grouped[:], "v3", "bank_c", nc.scalar.copy)
-        for j, grouped, copy in ((2, v2_grouped, nc.scalar.copy), (3, v3_grouped, nc.vector.tensor_copy)):
-            codes = sb.tile([P, P], U32, name="v%d_codes" % j, align_bytes=64)
-            scales = sb.tile([P, P], U8, name="v%d_scales" % j, align_bytes=64)
+        v3_turned = ps.tile([P, 2, P], F32, name="v3_turned", tag="bank_c")
+        for u in range(2):
+            nc.tensor.transpose(v3_turned[:, u, :], picked3[:, u:I // 2:2], ident[:])
+        pieces = [(2 * P, P, v2_grouped, "acc2", nc.scalar.copy)]
+        for first, bank, copy in ((0, "lower_bank", nc.vector.tensor_copy), (LAST, "size_rows", nc.scalar.copy)):
+            grouped = sb.tile([P, LAST, PACK], BF16, name="v3_grouped%d" % first, align_bytes=64)
+            nc.scalar.copy(out=grouped[:].bitcast(F32), in_=v3_turned[:, :, first:first + LAST].rearrange("p u r -> p r u"))
+            pieces.append((3 * P + first, LAST, grouped, bank, copy))
+        for first, width, grouped, bank, copy in pieces:
+            codes = sb.tile([P, width], U32, name="codes%d" % first, align_bytes=64)
+            scales = sb.tile([P, width], U8, name="scales%d" % first, align_bytes=64)
             quantize(grouped[:], codes[:], scales[:])
-            acc = ps.tile([Q, P], F32, name="acc%d" % j)
+            acc = ps.tile([Q, width], F32, name="acc%d" % first, tag=bank)
             product(acc[:], codes[:], scales[:])
-            res = sb.tile([Q, P], F32, name="res%d" % j)
-            store(j * P, acc, res, copy)
+            res = sb.tile([Q, width], F32, name="res%d" % first)
+            store(first, acc, res, copy)

@@ -17,6 +17,7 @@ ALU = mybir.AluOpType
 ACT = mybir.ActivationFunctionType
 P = 128
 PACK = 4
+BURST = 256
 POOL_BYTES = 4 * T
 AT_VALS = tuple(j * POOL_BYTES for j in range(4))
 AT_PICKED0 = 4 * POOL_BYTES
@@ -33,23 +34,23 @@ def tile_attend_multitoken_kernel(tc, query, keys_words, keys_scales, c0, c1, c2
         shared = ctx.enter_context(tc.tile_pool(name="shared", bufs=1))
         ps = ctx.enter_context(tc.psum_pool(name="ps", bufs=1))
 
-        q_raw = sb.tile([P, PACK, Q], F32, name="q_raw")
+        q_raw = sb.tile([P, PACK, Q], F32, name="q_raw", align_bytes=BURST)
         offsets = sb.tile([P, I // 16], U16, name="offsets")
         nc.sync.dma_start(out=q_raw[:], in_=query.rearrange("(p j) q -> p j q", j=PACK))
         nc.sync.dma_start(offsets[:], offs)
         c0_col = sb.tile([P, 1], F32, name="c0_col")
         nc.sync.dma_start(out=c0_col[:], in_=c0)
 
-        key_scales = sb.tile([P, T], U8, name="key_scales")
+        key_scales = sb.tile([P, T], U8, name="key_scales", align_bytes=BURST)
         nc.vector.memset(key_scales[:].bitcast(I32), 0)
         rows = keys_scales[0].rearrange("(g r) t -> r g t", r=4)
         for r in range(4):
             nc.sync.dma_start(out=key_scales[r:P:32, :].bitcast(I32), in_=rows[r].bitcast(I32))
-        key_words = sb.tile([P, T], U32, name="key_words")
+        key_words = sb.tile([P, T], U32, name="key_words", align_bytes=BURST)
         nc.sync.dma_start(out=key_words[:].bitcast(I32), in_=keys_words[0].rearrange("p n t -> p (n t)").bitcast(I32))
 
         ident = sb.tile([P, P], F32, name="ident")
-        small_rows = sb.tile([P, P], F32, name="small_rows")
+        small_rows = sb.tile([P, P], F32, name="small_rows", align_bytes=BURST)
         nc.vector.memset(small_rows[:], 0.0)
         nc.vector.memset(ident[:], 0.0)
         make_identity(nc, ident[:], nomemset=True)
@@ -58,7 +59,7 @@ def tile_attend_multitoken_kernel(tc, query, keys_words, keys_scales, c0, c1, c2
             nc.sync.dma_start(out=small_rows[row:row + 1, :], in_=src.rearrange("q o -> o q"))
         nc.sync.dma_start(out=small_rows[0:PACK, :], in_=size.rearrange("o (t j) -> (o t) j", t=PACK))
 
-        pools = [shared.tile([P, T], F32, name="vals%d" % j, offset=at) for j, at in enumerate(AT_VALS)]
+        pools = [shared.tile([P, T], F32, name="vals%d" % j, offset=at, align_bytes=BURST) for j, at in enumerate(AT_VALS)]
         for j, pool in enumerate(pools):
             nc.sync.dma_start(out=pool[:], in_=vals[j * P:(j + 1) * P, :])
 
@@ -149,7 +150,7 @@ def tile_attend_multitoken_kernel(tc, query, keys_words, keys_scales, c0, c1, c2
         picked3 = gather_values(3, sb.tile([P, I], BF16, name="picked3"), V3_ON_VECTOR)
         v2_grouped = shared.tile([P, P, PACK], BF16, name="v2_grouped", offset=AT_VALS[3] + 4 * 2 * P, align_bytes=64)
         turn(picked2, v2_grouped[:], "v2", "upper_bank", nc.vector.tensor_copy)
-        res01 = shared.tile([Q, 2 * P], F32, name="res01", offset=AT_VALS[3])
+        res01 = shared.tile([Q, 2 * P], F32, name="res01", offset=AT_VALS[3], align_bytes=BURST)
         store(0, acc01, res01, nc.scalar.copy)
         v3_turned = ps.tile([P, 2, P], F32, name="v3_turned", tag="bank_c")
         for u in range(2):
@@ -165,5 +166,5 @@ def tile_attend_multitoken_kernel(tc, query, keys_words, keys_scales, c0, c1, c2
             quantize(grouped[:], codes[:], scales[:])
             acc = ps.tile([Q, width], F32, name="acc%d" % first, tag=bank)
             product(acc[:], codes[:], scales[:])
-            res = sb.tile([Q, width], F32, name="res%d" % first)
+            res = sb.tile([Q, width], F32, name="res%d" % first, align_bytes=BURST)
             store(first, acc, res, copy)

@@ -21,6 +21,8 @@ BURST = 256
 POOL_BYTES = 4 * T
 AT_VALS = tuple(j * POOL_BYTES for j in range(4))
 AT_PICKED0 = 4 * POOL_BYTES
+AT_SMALL = AT_PICKED0 + 2 * I + 256
+PIECES = ((I // 2, I // 2), (I // 4, I // 4), (0, I // 4))
 C1_ROW, C2_ROW = 4, 5
 HALF = I // 2
 LAST = P // 2
@@ -50,7 +52,7 @@ def tile_attend_multitoken_kernel(tc, query, keys_words, keys_scales, c0, c1, c2
         nc.sync.dma_start(out=key_words[:].bitcast(I32), in_=keys_words[0].rearrange("p n t -> p (n t)").bitcast(I32))
 
         ident = sb.tile([P, P], F32, name="ident")
-        small_rows = sb.tile([P, P], F32, name="small_rows", align_bytes=BURST)
+        small_rows = shared.tile([P, P], F32, name="small_rows", offset=AT_SMALL, align_bytes=BURST)
         nc.vector.memset(small_rows[:], 0.0)
         nc.vector.memset(ident[:], 0.0)
         make_identity(nc, ident[:], nomemset=True)
@@ -81,44 +83,52 @@ def tile_attend_multitoken_kernel(tc, query, keys_words, keys_scales, c0, c1, c2
 
         q_grouped = sb.tile([P, Q, PACK], BF16, name="q_grouped", align_bytes=64)
         nc.scalar.copy(out=q_grouped[:], in_=q_raw[:].rearrange("p j q -> p q j"))
-        k_codes = sb.tile([P, I], U32, name="k_codes", align_bytes=64)
         k_scales = sb.tile([P, I], U8, name="k_scales", align_bytes=64)
         nc.vector.tensor_copy(k_scales[:], key_scales[:].indirect(offsets[:]))
         q_codes = sb.tile([P, Q], U32, name="q_codes", align_bytes=64)
         q_scales = sb.tile([P, Q], U8, name="q_scales", align_bytes=64)
         quantize(q_grouped[:], q_codes[:], q_scales[:])
         s = sb.tile([Q, I], F32, name="s")
-        scores, small_turned = {}, {}
-        for first, name in ((HALF, "upper_bank"), (0, "lower_bank")):
-            bank = ps.tile([Q, HALF + P], F32, name=name)
-            scores[first], small_turned[first] = bank[:, :HALF], bank[:, HALF:]
-            nc.tensor.transpose(small_turned[first], small_rows[:], ident[:])
-        for first in (HALF, 0):
-            nc.vector.tensor_copy(k_codes[:, first:first + HALF], key_words[:].indirect(offsets[:, first // 16:(first + HALF) // 16]))
-            nc.tensor.matmul_mx(out=scores[first], lhsT=q_codes[:].bitcast(FP8X4), lhsT_scale=q_scales[:],
-                                rhs=k_codes[:, first:first + HALF].bitcast(FP8X4), rhs_scale=k_scales[:, first:first + HALF],
+        upper_bank = ps.tile([Q, HALF + P], F32, name="upper_bank")
+        small_turned = upper_bank[:, HALF:]
+        nc.tensor.transpose(small_turned, small_rows[:], ident[:])
+        middle_bank = ps.tile([Q, P], F32, name="middle_bank")
+        lower_bank = ps.tile([Q, P], F32, name="lower_bank")
+        scores = (upper_bank[:, :HALF], middle_bank[:], lower_bank[:])
+        k_codes = (sb.tile([P, HALF], U32, name="k_upper", align_bytes=64),
+                   shared.tile([P, P], U32, name="k_middle", offset=AT_SMALL - 256, align_bytes=64),
+                   shared.tile([P, P], U32, name="k_lower", offset=AT_SMALL + 256, align_bytes=64))
+        small_cols = sb.tile([P, C2_ROW + 1], F32, name="small_cols")
+        for (first, n), codes, piece in zip(PIECES, k_codes, scores):
+            nc.vector.tensor_copy(codes[:], key_words[:].indirect(offsets[:, first // 16:(first + n) // 16]))
+            nc.tensor.matmul_mx(out=piece, lhsT=q_codes[:].bitcast(FP8X4), lhsT_scale=q_scales[:],
+                                rhs=codes[:].bitcast(FP8X4), rhs_scale=k_scales[:, first:first + n],
                                 start=True, stop=True)
-            nc.scalar.activation(out=s[:, first:first + HALF], in_=scores[first], func=ACT.Copy, scale=c0_col[:])
-        size_cols = sb.tile([P, PACK], F32, name="size_cols")
-        nc.scalar.copy(out=size_cols[:], in_=small_turned[0][:, :PACK])
+            nc.scalar.activation(out=s[:, first:first + n], in_=piece, func=ACT.Copy, scale=c0_col[:])
+            if first == HALF:
+                nc.scalar.copy(out=small_cols[:], in_=small_turned[:, :C2_ROW + 1])
         size_rows = ps.tile([Q, PACK, P], F32, name="size_rows")
         for t in range(PACK):
-            nc.tensor.transpose(size_rows[:, t, :], size_cols[:, t:t + 1].to_broadcast([P, P]), ident[:])
-        for k, row in ((1, C1_ROW), (2, C2_ROW)):
-            for first in (HALF, 0):
-                n = min(HALF, I - first - k)
-                nc.vector.scalar_tensor_tensor(out=s[:, first + k:first + k + n], in0=scores[first][:, :n], scalar=small_turned[first][:, row:row + 1],
-                                               in1=s[:, first + k:first + k + n], op0=ALU.mult, op1=ALU.add)
+            nc.tensor.transpose(size_rows[:, t, :], small_cols[:, t:t + 1].to_broadcast([P, P]), ident[:])
+        for j, k in ((0, 1), (1, 1), (0, 2), (2, 1), (1, 2), (2, 2)):
+            first, n = PIECES[j]
+            n = min(n, I - first - k)
+            row = C1_ROW + k - 1
+            nc.vector.scalar_tensor_tensor(out=s[:, first + k:first + k + n], in0=scores[j][:, :n], scalar=small_cols[:, row:row + 1],
+                                           in1=s[:, first + k:first + k + n], op0=ALU.mult, op1=ALU.add)
         neg_max = sb.tile([Q, 1], F32, name="neg_max")
         nc.vector.tensor_reduce(out=neg_max[:], in_=s[:], axis=mybir.AxisListType.X, op=ALU.max, negate=True)
         picked0 = gather_values(0, shared.tile([P, I], BF16, name="picked0", offset=AT_PICKED0), 0)
         v0_grouped = sb.tile([P, P, PACK], BF16, name="v0_grouped", align_bytes=64)
         turn(picked0, v0_grouped[:], "v0", "bank_c", nc.vector.tensor_copy)
+        v0_codes = sb.tile([P, P], U32, name="v0_codes", align_bytes=64)
+        v0_scales = sb.tile([P, P], U8, name="v0_scales", align_bytes=64)
         p = shared.tile([Q, I], F32, name="p", offset=AT_VALS[0])
         row_sum = sb.tile([Q, 1], F32, name="row_sum")
         nc.scalar.activation(out=p[:], in_=s[:], func=ACT.Exp, bias=neg_max[:], accum_out=row_sum[:])
         inv_sum = shared.tile([Q, 1], F32, name="inv_sum", offset=AT_PICKED0 + 32)
         nc.vector.reciprocal(out=inv_sum[:], in_=row_sum[:])
+        quantize(v0_grouped[:], v0_codes[:], v0_scales[:])
         w = sb.tile([Q, I], BF16, name="w")
         nc.vector.scalar_tensor_tensor(out=w[:], in0=p[:],
                                        scalar=inv_sum[:], in1=size_rows[:].rearrange("q t j -> q (t j)"),
@@ -129,13 +139,12 @@ def tile_attend_multitoken_kernel(tc, query, keys_words, keys_scales, c0, c1, c2
         v1_grouped = sb.tile([P, P, PACK], BF16, name="v1_grouped", align_bytes=64)
         turn(picked1, v1_grouped[:], "v1", "size_rows", nc.scalar.copy)
         picked2 = gather_values(2, sb.tile([P, I], BF16, name="picked2"), I)
-        v01_codes = shared.tile([P, 2 * P], U32, name="v01_codes", offset=AT_VALS[2], align_bytes=64)
-        v01_scales = sb.tile([P, 2 * P], U8, name="v01_scales", align_bytes=64)
+        v1_codes = shared.tile([P, P], U32, name="v1_codes", offset=AT_VALS[2], align_bytes=64)
+        v1_scales = sb.tile([P, P], U8, name="v1_scales", align_bytes=64)
         w_codes = shared.tile([P, Q], U32, name="w_codes", offset=AT_VALS[2] + 4 * 2 * P, align_bytes=64)
         w_scales = sb.tile([P, Q], U8, name="w_scales", align_bytes=64)
-        quantize(v0_grouped[:], v01_codes[:, :P], v01_scales[:, :P])
         quantize(w_grouped[:], w_codes[:], w_scales[:])
-        quantize(v1_grouped[:], v01_codes[:, P:], v01_scales[:, P:])
+        quantize(v1_grouped[:], v1_codes[:], v1_scales[:])
 
         def product(acc, codes, scales):
             nc.tensor.matmul_mx(out=acc, lhsT=w_codes[:].bitcast(FP8X4), lhsT_scale=w_scales[:],
@@ -146,7 +155,8 @@ def tile_attend_multitoken_kernel(tc, query, keys_words, keys_scales, c0, c1, c2
             nc.sync.dma_start(out=out[:, first:first + res.shape[1]], in_=res[:])
 
         acc01 = ps.tile([Q, 2 * P], F32, name="acc01")
-        product(acc01[:], v01_codes[:], v01_scales[:])
+        product(acc01[:, :P], v0_codes[:], v0_scales[:])
+        product(acc01[:, P:], v1_codes[:], v1_scales[:])
         picked3 = gather_values(3, sb.tile([P, I], BF16, name="picked3"), V3_ON_VECTOR)
         v2_grouped = shared.tile([P, P, PACK], BF16, name="v2_grouped", offset=AT_VALS[3] + 4 * 2 * P, align_bytes=64)
         turn(picked2, v2_grouped[:], "v2", "upper_bank", nc.vector.tensor_copy)

@@ -27,6 +27,7 @@ C1_ROW, C2_ROW = 4, 5
 HALF = I // 2
 LAST = P // 2
 V3_ON_VECTOR = 256
+FIRST_STORE_ROWS = ((0, 32), (32, 32), (64, 32), (96, 16), (112, 16))
 
 
 def tile_attend_multitoken_kernel(tc, query, keys_words, keys_scales, c0, c1, c2, size, vals, offs, out):
@@ -161,7 +162,9 @@ def tile_attend_multitoken_kernel(tc, query, keys_words, keys_scales, c0, c1, c2
         v2_grouped = shared.tile([P, P, PACK], BF16, name="v2_grouped", offset=AT_VALS[3] + 4 * 2 * P, align_bytes=64)
         turn(picked2, v2_grouped[:], "v2", "upper_bank", nc.vector.tensor_copy)
         res01 = shared.tile([Q, 2 * P], F32, name="res01", offset=AT_VALS[3], align_bytes=BURST)
-        store(0, acc01, res01, nc.scalar.copy)
+        nc.scalar.copy(out=res01[:], in_=acc01[:])
+        for first, n in FIRST_STORE_ROWS:
+            nc.sync.dma_start(out=out[first:first + n, :2 * P], in_=res01[first:first + n, :])
         v3_turned = ps.tile([P, 2, P], F32, name="v3_turned", tag="bank_c")
         for u in range(2):
             nc.tensor.transpose(v3_turned[:, u, :], picked3[:, u:I // 2:2], ident[:])

from contextlib import ExitStack

import concourse.mybir as mybir
from concourse.masks import make_identity

D, T, I, Q, E = 512, 2048, 512, 128, 512
FLOPS = 2 * D * Q * I + 2 * I * Q * E

F32 = mybir.dt.float32
BF16 = mybir.dt.bfloat16
I32 = mybir.dt.int32
U32 = mybir.dt.uint32
U16 = mybir.dt.uint16
U8 = mybir.dt.uint8
FP8X4 = mybir.dt.float8_e4m3fn_x4
ALU = mybir.AluOpType
ACT = mybir.ActivationFunctionType
P = 128
PACK = 4
BURST = 256
POOL_BYTES = 4 * T
AT_VALS = tuple(j * POOL_BYTES for j in range(4))
AT_PICKED0 = 4 * POOL_BYTES
AT_SMALL = AT_PICKED0 + 2 * I + 256
PIECES = ((I // 2, I // 2), (I // 4, I // 4), (0, I // 4))
C1_ROW, C2_ROW = 4, 5
HALF = I // 2
LAST = P // 2
V3_ON_VECTOR = 256
FIRST_STORE_ROWS = ((0, 32), (32, 32), (64, 32), (96, 16), (112, 16))


def tile_attend_multitoken_kernel(tc, query, keys_words, keys_scales, c0, c1, c2, size, vals, offs, out):
    nc = tc.nc
    with ExitStack() as ctx:
        sb = ctx.enter_context(tc.tile_pool(name="sb", bufs=1))
        shared = ctx.enter_context(tc.tile_pool(name="shared", bufs=1))
        ps = ctx.enter_context(tc.psum_pool(name="ps", bufs=1))

        q_raw = sb.tile([P, PACK, Q], F32, name="q_raw", align_bytes=BURST)
        offsets = sb.tile([P, I // 16], U16, name="offsets")
        nc.sync.dma_start(out=q_raw[:], in_=query.rearrange("(p j) q -> p j q", j=PACK))
        nc.sync.dma_start(offsets[:], offs)
        c0_col = sb.tile([P, 1], F32, name="c0_col")
        nc.sync.dma_start(out=c0_col[:], in_=c0)

        key_scales = sb.tile([P, T], U8, name="key_scales", align_bytes=BURST)
        nc.vector.memset(key_scales[:].bitcast(I32), 0)
        rows = keys_scales[0].rearrange("(g r) t -> r g t", r=4)
        for r in range(4):
            nc.sync.dma_start(out=key_scales[r:P:32, :].bitcast(I32), in_=rows[r].bitcast(I32))
        key_words = sb.tile([P, T], U32, name="key_words", align_bytes=BURST)
        nc.sync.dma_start(out=key_words[:].bitcast(I32), in_=keys_words[0].rearrange("p n t -> p (n t)").bitcast(I32))

        ident = sb.tile([P, P], F32, name="ident")
        small_rows = shared.tile([P, P], F32, name="small_rows", offset=AT_SMALL, align_bytes=BURST)
        nc.vector.memset(small_rows[:], 0.0)
        nc.vector.memset(ident[:], 0.0)
        make_identity(nc, ident[:], nomemset=True)

        for row, src in ((C1_ROW, c1), (C2_ROW, c2)):
            nc.sync.dma_start(out=small_rows[row:row + 1, :], in_=src.rearrange("q o -> o q"))
        nc.sync.dma_start(out=small_rows[0:PACK, :], in_=size.rearrange("o (t j) -> (o t) j", t=PACK))

        pools = [shared.tile([P, T], F32, name="vals%d" % j, offset=at, align_bytes=BURST) for j, at in enumerate(AT_VALS)]
        for j, pool in enumerate(pools):
            nc.sync.dma_start(out=pool[:], in_=vals[j * P:(j + 1) * P, :])

        def quantize(grouped, codes, scales):
            nc.vector.quantize_mx(out=codes.bitcast(FP8X4), scales=scales, in_=grouped.rearrange("p w j -> p (w j)"))

        def turn(words, grouped, name, bank, copy):
            turned = ps.tile([P, 2, P], F32, name=name + "_turned", tag=bank)
            for u in range(2):
                nc.tensor.transpose(turned[:, u, :], words[:, u:I // 2:2], ident[:])
            copy(out=grouped.bitcast(F32), in_=turned[:].rearrange("p u r -> p r u"))

        def gather_values(j, picked, on_vector):
            if on_vector > 0:
                nc.vector.tensor_copy(picked[:, :on_vector], pools[j][:].indirect(offsets[:, :on_vector // 16]))
            if on_vector < I:
                nc.scalar.activation(out=picked[:, on_vector:], in_=pools[j][:].indirect(offsets[:, on_vector // 16:]), func=ACT.Copy)
            return picked[:].bitcast(F32)

        q_grouped = sb.tile([P, Q, PACK], BF16, name="q_grouped", align_bytes=64)
        nc.scalar.copy(out=q_grouped[:], in_=q_raw[:].rearrange("p j q -> p q j"))
        k_scales = sb.tile([P, I], U8, name="k_scales", align_bytes=64)
        nc.vector.tensor_copy(k_scales[:], key_scales[:].indirect(offsets[:]))
        q_codes = sb.tile([P, Q], U32, name="q_codes", align_bytes=64)
        q_scales = sb.tile([P, Q], U8, name="q_scales", align_bytes=64)
        quantize(q_grouped[:], q_codes[:], q_scales[:])
        s = sb.tile([Q, I], F32, name="s")
        upper_bank = ps.tile([Q, HALF + P], F32, name="upper_bank")
        small_turned = upper_bank[:, HALF:]
        nc.tensor.transpose(small_turned, small_rows[:], ident[:])
        middle_bank = ps.tile([Q, P], F32, name="middle_bank")
        lower_bank = ps.tile([Q, P], F32, name="lower_bank")
        scores = (upper_bank[:, :HALF], middle_bank[:], lower_bank[:])
        k_codes = (sb.tile([P, HALF], U32, name="k_upper", align_bytes=64),
                   shared.tile([P, P], U32, name="k_middle", offset=AT_SMALL - 256, align_bytes=64),
                   shared.tile([P, P], U32, name="k_lower", offset=AT_SMALL + 256, align_bytes=64))
        small_cols = sb.tile([P, C2_ROW + 1], F32, name="small_cols")
        for (first, n), codes, piece in zip(PIECES, k_codes, scores):
            nc.vector.tensor_copy(codes[:], key_words[:].indirect(offsets[:, first // 16:(first + n) // 16]))
            nc.tensor.matmul_mx(out=piece, lhsT=q_codes[:].bitcast(FP8X4), lhsT_scale=q_scales[:],
                                rhs=codes[:].bitcast(FP8X4), rhs_scale=k_scales[:, first:first + n],
                                start=True, stop=True)
            nc.scalar.activation(out=s[:, first:first + n], in_=piece, func=ACT.Copy, scale=c0_col[:])
            if first == HALF:
                nc.scalar.copy(out=small_cols[:], in_=small_turned[:, :C2_ROW + 1])
        size_rows = ps.tile([Q, PACK, P], F32, name="size_rows")
        for t in range(PACK):
            nc.tensor.transpose(size_rows[:, t, :], small_cols[:, t:t + 1].to_broadcast([P, P]), ident[:])
        for j, k in ((0, 1), (1, 1), (0, 2), (2, 1), (1, 2), (2, 2)):
            first, n = PIECES[j]
            n = min(n, I - first - k)
            row = C1_ROW + k - 1
            nc.vector.scalar_tensor_tensor(out=s[:, first + k:first + k + n], in0=scores[j][:, :n], scalar=small_cols[:, row:row + 1],
                                           in1=s[:, first + k:first + k + n], op0=ALU.mult, op1=ALU.add)
        neg_max = sb.tile([Q, 1], F32, name="neg_max")
        nc.vector.tensor_reduce(out=neg_max[:], in_=s[:], axis=mybir.AxisListType.X, op=ALU.max, negate=True)
        picked0 = gather_values(0, shared.tile([P, I], BF16, name="picked0", offset=AT_PICKED0), 0)
        v0_grouped = sb.tile([P, P, PACK], BF16, name="v0_grouped", align_bytes=64)
        turn(picked0, v0_grouped[:], "v0", "bank_c", nc.vector.tensor_copy)
        v0_codes = sb.tile([P, P], U32, name="v0_codes", align_bytes=64)
        v0_scales = sb.tile([P, P], U8, name="v0_scales", align_bytes=64)
        p = shared.tile([Q, I], F32, name="p", offset=AT_VALS[0])
        row_sum = sb.tile([Q, 1], F32, name="row_sum")
        nc.scalar.activation(out=p[:], in_=s[:], func=ACT.Exp, bias=neg_max[:], accum_out=row_sum[:])
        inv_sum = shared.tile([Q, 1], F32, name="inv_sum", offset=AT_PICKED0 + 32)
        nc.vector.reciprocal(out=inv_sum[:], in_=row_sum[:])
        quantize(v0_grouped[:], v0_codes[:], v0_scales[:])
        w = sb.tile([Q, I], BF16, name="w")
        nc.vector.scalar_tensor_tensor(out=w[:], in0=p[:],
                                       scalar=inv_sum[:], in1=size_rows[:].rearrange("q t j -> q (t j)"),
                                       op0=ALU.mult, op1=ALU.mult)
        picked1 = gather_values(1, sb.tile([P, I], BF16, name="picked1"), 0)
        w_grouped = shared.tile([P, Q, PACK], BF16, name="w_grouped", offset=AT_VALS[1], align_bytes=64)
        turn(w[:].bitcast(F32), w_grouped[:], "w", "lower_bank", nc.scalar.copy)
        v1_grouped = sb.tile([P, P, PACK], BF16, name="v1_grouped", align_bytes=64)
        turn(picked1, v1_grouped[:], "v1", "size_rows", nc.scalar.copy)
        picked2 = gather_values(2, sb.tile([P, I], BF16, name="picked2"), I)
        v1_codes = shared.tile([P, P], U32, name="v1_codes", offset=AT_VALS[2], align_bytes=64)
        v1_scales = sb.tile([P, P], U8, name="v1_scales", align_bytes=64)
        w_codes = shared.tile([P, Q], U32, name="w_codes", offset=AT_VALS[2] + 4 * 2 * P, align_bytes=64)
        w_scales = sb.tile([P, Q], U8, name="w_scales", align_bytes=64)
        quantize(w_grouped[:], w_codes[:], w_scales[:])
        quantize(v1_grouped[:], v1_codes[:], v1_scales[:])

        def product(acc, codes, scales):
            nc.tensor.matmul_mx(out=acc, lhsT=w_codes[:].bitcast(FP8X4), lhsT_scale=w_scales[:],
                                rhs=codes.bitcast(FP8X4), rhs_scale=scales, start=True, stop=True)

        def store(first, acc, res, copy):
            copy(out=res[:], in_=acc[:])
            nc.sync.dma_start(out=out[:, first:first + res.shape[1]], in_=res[:])

        acc01 = ps.tile([Q, 2 * P], F32, name="acc01")
        product(acc01[:, :P], v0_codes[:], v0_scales[:])
        product(acc01[:, P:], v1_codes[:], v1_scales[:])
        picked3 = gather_values(3, sb.tile([P, I], BF16, name="picked3"), V3_ON_VECTOR)
        v2_grouped = shared.tile([P, P, PACK], BF16, name="v2_grouped", offset=AT_VALS[3] + 4 * 2 * P, align_bytes=64)
        turn(picked2, v2_grouped[:], "v2", "upper_bank", nc.vector.tensor_copy)
        res01 = shared.tile([Q, 2 * P], F32, name="res01", offset=AT_VALS[3], align_bytes=BURST)
        nc.scalar.copy(out=res01[:], in_=acc01[:])
        for first, n in FIRST_STORE_ROWS:
            nc.sync.dma_start(out=out[first:first + n, :2 * P], in_=res01[first:first + n, :])
        v3_turned = ps.tile([P, 2, P], F32, name="v3_turned", tag="bank_c")
        for u in range(2):
            nc.tensor.transpose(v3_turned[:, u, :], picked3[:, u:I // 2:2], ident[:])
        pieces = [(2 * P, P, v2_grouped, "acc2", nc.scalar.copy)]
        for first, bank, copy in ((0, "lower_bank", nc.vector.tensor_copy), (LAST, "size_rows", nc.scalar.copy)):
            grouped = sb.tile([P, LAST, PACK], BF16, name="v3_grouped%d" % first, align_bytes=64)
            nc.scalar.copy(out=grouped[:].bitcast(F32), in_=v3_turned[:, :, first:first + LAST].rearrange("p u r -> p r u"))
            pieces.append((3 * P + first, LAST, grouped, bank, copy))
        for first, width, grouped, bank, copy in pieces:
            codes = sb.tile([P, width], U32, name="codes%d" % first, align_bytes=64)
            scales = sb.tile([P, width], U8, name="scales%d" % first, align_bytes=64)
            quantize(grouped[:], codes[:], scales[:])
            acc = ps.tile([Q, width], F32, name="acc%d" % first, tag=bank)
            product(acc[:], codes[:], scales[:])
            res = sb.tile([Q, width], F32, name="res%d" % first, align_bytes=BURST)
            store(first, acc, res, copy)
